import numpy as np, ml_dtypes
CORES = [6,15,38,47]
N = 4
BF = ml_dtypes.bfloat16
def gentries(a):
    return np.ascontiguousarray(a.reshape(8, 16, -1).transpose(0, 2, 1)).reshape(8, -1)
def gtable(e):
    e = np.asarray(e); return np.ascontiguousarray(e.reshape(8, -1, 16).transpose(0, 2, 1)).reshape(128, -1).astype(np.int32)
R, A, J, W, Q, SH, RO = 64, 8, 4, 4096, 28, 4, 4
def parts(rng):
    amp = rng.choice(np.array([16, 32, 64, 128]), (N, 8, 1, 1))
    p = (amp * rng.random((N, 8, 16, W))).astype(np.int64)
    s = rng.integers(0, 1009, (N, 8, 1, W)) + rng.integers(0, 16, (N, 8, 16, W))
    c = rng.integers(0, W, (N, 8, R, Q)); nbr = rng.integers(0, N * R, (N, 8, J, R)); ge = rng.integers(0, W, (N, 8, J, R))
    return p, s, c, nbr, ge
def pack(p, s, c, nbr, ge):
    return {"pe": np.ascontiguousarray(p.reshape(N, 128, W)).astype(np.float32).astype(BF), "se": np.ascontiguousarray(s.reshape(N, 128, W)).astype(np.int32),
            "cand": np.ascontiguousarray(c.reshape(N, 8, R * Q)).astype(np.int32),
            "nb": np.stack([gtable(a.reshape(8, -1)) for a in nbr]), "geo": np.stack([gtable(a.reshape(8, -1)) for a in ge])}
def setup_inputs(rng):
    return pack(*parts(rng))
def ladder():
    o = [512 + 8 * (A - 1 - a) for a in range(A)]
    w = [0] * A
    for i in range(A // 2):
        w[(A - 1 + 2 * i) % A] = 512 - 8 * i; w[2 * i] = 200 + 8 * (A // 2 - 1 - i)
    o += w[:A - 1]
    h = 512 - 8 * (A // 2 - 1); ch = [(A - 3 + 3 * i) % A for i in range(A)]; m = ch.index(A - 2)
    for i in range(A): w[ch[i]] = h - (h - 200) * i // m if i < m else 200 - 8 * (i - m)
    return np.array(o + w[:A - 3] + [w[A - 1]])
def setup_inputs_most(rng):
    p, s, c, nbr, ge = parts(rng); o = ladder(); k = W // 1024
    for q in range(N):
        for g in range(8):
            pm = rng.permutation(W); lv = np.zeros(W, np.int64); lv[pm] = np.arange(W) // k
            s[q, g] = lv[None, :]; p[q, g] = rng.integers(0, 2, (16, W))
            v = rng.integers(0, 1024, (R, Q)); v[:, :len(o)] = o[None, :] + rng.integers(-100, 301, (R, 1))
            c[q, g] = pm[v * k + rng.integers(0, k, (R, Q))]
    far = 1 + rng.permutation(N) % (N - 1)
    nbr = ((np.arange(N) + far) % N * R)[:, None, None, None] + rng.integers(0, R, (N, 8, J, R))
    return pack(p, s, c, nbr, ge)
def setup_inputs_ties(rng):
    p, s, c, nbr, ge = parts(rng)
    p[:, ::2] = rng.integers(0, 128, (N, 4, 16, 1)); p[:, 1::2] = rng.integers(0, 2, (N, 4, 16, W))
    lv = rng.integers(0, 4, (N, 8, 1, W)); lv[:, 1::2] = rng.integers(0, 12, (N, 4, 1, W))
    lone = rng.integers(0, 64, (N, 8, 1, W)) == np.arange(16)[:, None]
    s = 1 + lv + rng.integers(0, 900, (N, 8, 16, 1)) - lone
    return pack(p, s, c, nbr, ge)
def setup_inputs_ends(rng):
    p, s, c, nbr, ge = parts(rng)
    c[:, ::2] = rng.choice(np.array([0, 1, W // 2 - 1, W - 5, W - 3, W - 1]), (N, 4, R, Q)); ge[:, ::2] = rng.choice(np.array([0, 1, W - 1]), (N, 4, J, R))
    s[:, ::2, :, 0] = 0; s[:, ::2, :, W - 1] = 1023; s[:, ::2, :, W // 2 - 1] = 500
    p[:, ::4] = 127 * rng.integers(0, 2, (N, 2, 16, W))
    own = np.arange(N)[:, None, None] * R
    nbr[:, 0] = own + np.arange(R)
    nbr[:, 1] = rng.choice(np.array([0, R - 1, (N - 1) * R, N * R - 1]), (N, J, R))
    nbr[:, 3] = rng.integers(0, N * R, (N, 1, R))
    nbr[:, 5] = (own + R) % (N * R) + rng.integers(0, R, (N, J, R))
    nbr[:, 7] = own + rng.integers(0, R, (N, J, R))
    return pack(p, s, c, nbr, ge)
def setup_inputs_still(rng):
    p, s, c, nbr, ge = parts(rng); o = rng.permutation(8); b, h = o[4], o[5]
    c[:, o[4:6], ::4] = 1 << SH; nbr[:, o[4:6]] = 4 * rng.integers(0, N * R // 4, (N, 2, J, R)); ge[:, o[4:6]] = 64 * rng.integers(0, W // 64, (N, 2, J, R))
    p[:, b] = np.tile(rng.integers(0, 128, (N, 16, 64)), (1, 1, W // 64))
    s[:, b] = rng.integers(127 * J, 1016, (N, 1, W)) - J * p[:, b] + rng.integers(0, 8, (N, 16, W))
    t = np.tile(np.argsort(rng.random((N, 1, 64)), axis=-1) & 1, (1, 1, W // 64)); one = np.arange(16)[:, None] == rng.integers(0, 16, (N, 1, 1))
    p[:, h] = np.where(one, 127 * (1 - t), np.tile(rng.integers(0, 128, (N, 16, 64)), (1, 1, W // 64)))
    s[:, h] = 127 * J - J * p[:, h] + np.where(one, rng.integers(0, 101, (N, 1, 1)) + rng.integers(0, 3, (N, 1, W)), rng.integers(0, 56, (N, 1, W)) + 64 * t + rng.integers(0, 8, (N, 16, W)))
    q = int(rng.integers(0, N)); p[q] = rng.integers(0, 128, (8, 16, W)); s[q] = s[q] >> 5
    p[:, o[0]] = rng.integers(0, 128, (N, 16, 1)); s[:, o[0]] = rng.integers(0, 1024, (N, 16, 1))
    lv = rng.integers(0, 1024, (N, 1, W)); p[:, o[1]] = rng.integers(0, 2, (N, 16, W)); s[:, o[1]] = lv; s[:, o[1], int(rng.integers(0, 16))] = 1023 - lv[:, 0]
    for a in range(N):
        for g, sign in ((o[2], 1), (o[3], -1)):
            i = np.argsort(sign * s[a, g, 0][c[a, g]], axis=-1); c[a, g] = np.take_along_axis(c[a, g], i, -1)
    return pack(p, s, c, nbr, ge)
def setup_inputs_spread(rng):
    p, s, c, nbr, ge = parts(rng)
    p = np.minimum((np.exp2(7 * rng.random((N, 8, 1, W))) * rng.random((N, 8, 16, W))).astype(np.int64), 127)
    s = np.minimum((np.exp2(10 * rng.random((N, 8, 1, W))) * (0.875 + 0.125 * rng.random((N, 8, 16, W)))).astype(np.int64), 1023)
    e = rng.choice(np.array([1.0, 2.0, 4.0]), (N, 8, 1, 1))
    c = np.minimum((W * rng.random((N, 8, R, Q)) ** e).astype(np.int64), W - 1)
    nbr = np.minimum((N * R * rng.random((N, 8, J, R)) ** 2).astype(np.int64), N * R - 1)
    ge = np.minimum((W * rng.random((N, 8, J, R)) ** e).astype(np.int64), W - 1)
    return pack(p, s, c, nbr, ge)
def check_inputs(d):
    bad = []
    v = np.asarray(d["pe"]).astype(np.float32)
    if not (np.all(v >= 0) and np.all(v <= 127) and np.all(v == np.floor(v))): bad.append("range of pe")
    for k, hi in (("se", 1023), ("cand", W - 1), ("nb", N * R - 1), ("geo", W - 1)):
        if np.min(d[k]) < 0 or np.max(d[k]) > hi: bad.append("range of " + k)
    return bad
def reference(pe, se, cand, nb, geo):
    p = pe.astype(np.float32).astype(np.int32).reshape(N, 8, 16, W); s = se.astype(np.int32).reshape(N, 8, 16, W)
    qu = cand.astype(np.int64).reshape(N, 8, R, Q)
    nbl = np.stack([gentries(a) for a in nb]).astype(np.int64).reshape(N, 8, J, R); ge = np.stack([gentries(a) for a in geo]).astype(np.int64).reshape(N, 8, J, R)
    pos = np.zeros((N, 8, R, A), np.int64) + np.arange(A); head = np.full((N, 8, R, 1), A, np.int64)
    for t in range(RO):
        c = np.take_along_axis(qu, pos, 3)
        every = c.transpose(1, 0, 2, 3).reshape(8, N * R, A)
        gap = []
        for a in range(N):
            cu = every[np.arange(8)[:, None, None], nbl[a]]
            ix = (((c[a][:, None, :, :, None] * cu[:, :, :, None, :]) >> SH) + ge[a][:, :, :, None, None]) & (W - 1)
            e = np.take_along_axis(p[a], ix.reshape(8, 1, -1), 2).reshape(8, 16, J, R, A, A)
            low = np.min(e - np.roll(e, -(t + 1), axis=4), axis=5)
            own = np.take_along_axis(s[a], c[a].reshape(8, 1, -1), 2).reshape(8, 16, R, A)
            gap.append(own - np.roll(own, -(t + 1), axis=3) + np.add.reduce(low, axis=2))
        gap = np.stack(gap)
        dead = np.all(gap > 0, axis=2)
        if t < RO - 1:
            n = dead.astype(np.int64); upto = np.add.accumulate(n, axis=3)
            pos = np.where(dead, head + upto - n, pos); head = head + upto[..., -1:]
    return {"yc": np.where(dead, -1, c).reshape(N, 8, R * A).astype(np.float32), "yg": gap.reshape(N, 128, R * A).astype(np.float32)}

@@ -1,0 +1,510 @@
+from concourse.bass import DstId, RemoteDMATransfer
+from concourse.mybir import AluOpType, ActivationFunctionType
+
+BF, F32, I32, U16 = "bfloat16", "float32", "int32", "uint16"
+NCH = 4
+BIG = 1024.0
+SCRATCH = {
+    "pw": ("sbuf", [128, 4096], BF), "sw": ("sbuf", [128, 4096], I32), "sq": ("sbuf", [128, 1792], F32),
+    "cq": ("sbuf", [128, 1792], BF),
+    "candl": ("sbuf", [128, 112], I32), "clo": ("sbuf", [128, 112], I32), "clob": ("sbuf", [128, 112], BF),
+    "chib": ("sbuf", [128, 112], BF), "cand16": ("sbuf", [128, 112], U16),
+    "nbi": ("sbuf", [128, 16], I32), "nbu": ("sbuf", [128, 16], U16), "geoi": ("sbuf", [128, 16], I32),
+    "geof": ("sbuf", [128, 16], F32), "gm": ("sbuf", [128, 256], F32), "geor": ("sbuf", [128, 16, 4, 16], F32),
+    "w0": ("sbuf", [128, 256], F32), "w1": ("sbuf", [128, 256], F32), "w2": ("sbuf", [128, 256], F32), "w3": ("sbuf", [128, 256], F32),
+    "ones": ("sbuf", [128, 128], BF), "ip": ("sbuf", [128, 128], BF), "im": ("sbuf", [128, 128], BF),
+    "bt": ("sbuf", [128, 128], BF), "bm": ("sbuf", [128, 128], BF), "bf32": ("sbuf", [128, 128], F32), "bn": ("sbuf", [128, 128], BF),
+    "kc": ("sbuf", [128, 128], BF), "selk": ("sbuf", [128, 64, 2], BF), "csel": ("sbuf", [128, 8, 8, 8, 2], BF), "casel": ("sbuf", [128, 2, 64, 2], BF),
+    "thr": ("sbuf", [128, 128], F32), "qrow": ("sbuf", [128, 128], F32), "m16": ("sbuf", [128, 16], F32),
+    "rt0": ("sbuf", [128, 24], BF), "rt1": ("sbuf", [128, 24], BF), "rt2": ("sbuf", [128, 24], BF),
+    "rmin": ("sbuf", [128, 512], BF), "rmax": ("sbuf", [128, 512], BF),
+    "ci": ("sbuf", [128, 16], I32), "cf": ("sbuf", [128, 16], F32),
+    "posc": ("sbuf", [128, 32], F32), "headc": ("sbuf", [128, 32], F32), "sbase": ("sbuf", [128, 32], F32), "sbf": ("sbuf", [128, 32], F32),
+    "t1": ("sbuf", [128, 8], F32), "t3": ("sbuf", [128, 8], F32), "offc": ("sbuf", [128, 32], U16), "offs": ("sbuf", [128, 32], U16),
+    "crow": ("sbuf", [128, 4, 128], BF), "own": ("sbuf", [128, 512], F32), "ns": ("sbuf", [128, 4, 8, 16], F32), "cr": ("sbuf", [128, 4, 8, 16], F32),
+    "cn": ("sbuf", [128, 256], F32), "idx": ("sbuf", [128, 16, 4, 16], I32), "off": ("sbuf", [128, 1024], U16),
+    "flg": ("sbuf", [128, 128], BF), "dm": ("sbuf", [128, 128], BF),
+    "ygb": ("sbuf", [128, 64, 8], F32), "ycb": ("sbuf", [128, 64, 8], F32),
+    "fa": ("sbuf", [128, 512], BF), "fb": ("sbuf", [128, 512], BF),
+    "d0": ("psum", [128, 512], F32), "d1": ("psum", [128, 512], F32), "d2": ("psum", [128, 512], F32), "d3": ("psum", [128, 512], F32),
+    "ca0": ("psum", [128, 2, 4, 64], F32), "ca1": ("psum", [128, 2, 4, 64], F32),
+    "jb": ("psum", [128, 4, 8, 16], F32), "mb": ("psum", [128, 4, 128], F32),
+}
+for _c in range(NCH):
+    SCRATCH["e%d" % _c] = ("sbuf", [128, 4096], BF)
+    SCRATCH["sc%d" % _c] = ("sbuf", [128, 8, 512], BF)
+NDMA = 12
+SEMAPHORES = ["sV", "sS", "sP", "sG", "loc"] + ["arr%d" % i for i in range(4)] + ["dma%d" % i for i in range(NDMA)]
+
+
+def slot(t, al, b):
+    s = t + 1
+    if s in (2, 4):
+        return 2 * al + b
+    return (s * al + 4 * b) % 8
+
+
+def rank_program(g, core, T, topo):
+    rank = T.rank_of(core)
+    if rank is None:
+        return
+    A = AluOpType
+    COPY = ActivationFunctionType.Copy
+    V, S, P = g.vector, g.scalar, g.tensor
+    queue = {"V": V, "S": S, "P": P, "G": g, "Y": g.sync}
+    count = {"sV": 0, "sS": 0, "sP": 0, "sG": 0}
+    know = {e: {} for e in queue}
+    snaps = {}
+    wr, rd, bank = {}, {}, {}
+    ndma = [0]
+
+    def need(e, tokens):
+        todo = {}
+        for sem, val in tokens:
+            if know[e].get(sem, 0) < val:
+                todo[sem] = max(todo.get(sem, 0), val)
+        items = sorted(todo.items(), key=lambda it: -sum(snaps[it].values()))
+        for sem, val in items:
+            if know[e].get(sem, 0) >= val:
+                continue
+            queue[e].wait_ge(T.sem[sem], val)
+            for k, v in snaps[(sem, val)].items():
+                know[e][k] = max(know[e].get(k, 0), v)
+            know[e][sem] = max(know[e].get(sem, 0), val)
+
+    def deps(e, r, w, x):
+        own = "s" + e
+        tok = []
+        for k in r:
+            if k in wr:
+                tok.append(wr[k])
+        for k in w:
+            if k in wr:
+                tok.append(wr[k])
+            for q in rd.get(k, ()):
+                if q[0] != own:
+                    tok.append(q)
+        for k in x:
+            for q in bank.get(k, {}).values():
+                if q[0] != own:
+                    tok.append(q)
+        return tok
+
+    def mark(tok, r, w, x):
+        for k in r:
+            lst = [q for q in rd.get(k, []) if q[0] != tok[0]]
+            lst.append(tok)
+            rd[k] = lst
+        for k in w:
+            wr[k] = tok
+            rd[k] = []
+        for k in x:
+            bank.setdefault(k, {})[tok[0]] = tok
+
+    def op(e, calls, r=(), w=(), x=()):
+        need(e, deps(e, r, w, x))
+        sem = "s" + e
+        for call in (calls if isinstance(calls, list) else [calls]):
+            call().then_inc(T.sem[sem], 1)
+            count[sem] += 1
+        tok = (sem, count[sem])
+        sn = dict(know[e])
+        sn[sem] = count[sem]
+        snaps[tok] = sn
+        mark(tok, r, w, x)
+
+    def dma(e, out, in_, r=(), w=()):
+        need(e, deps("dma", r, w, ()))
+        sem = "dma%d" % ndma[0]
+        ndma[0] += 1
+        queue[e].dma_start(out, in_).then_inc(T.sem[sem], 16)
+        tok = (sem, 16)
+        sn = dict(know[e])
+        sn[sem] = 16
+        snaps[tok] = sn
+        mark(tok, r, w, ())
+
+    W = [T.w0, T.w1, T.w2, T.w3]
+    D = [T.d0, T.d1, T.d2, T.d3]
+    E = [T["e%d" % c] for c in range(NCH)]
+    SC = [T["sc%d" % c] for c in range(NCH)]
+    RT = [T.rt0, T.rt1, T.rt2]
+    CA = [T.ca0, T.ca1]
+    others = [c for c in T.cores if c != core]
+
+    def ts(out, in0, s1, op0, s2=None, op1=None):
+        if op1 is None:
+            return lambda: V.tensor_scalar(out, in0, s1, None, op0)
+        return lambda: V.tensor_scalar(out, in0, s1, s2, op0, op1)
+
+    def tt(out, a, b, o):
+        return lambda: V.tensor_tensor(out, a, b, o)
+
+    def cp(out, a):
+        return lambda: V.tensor_copy(out, a)
+
+    def ms(out, v):
+        return lambda: V.memset(out, v)
+
+    def mm(out, l, rhs, st, sp):
+        return lambda: P.matmul(out, l, rhs, st, sp)
+
+    dma("Y", T.candl[:], T.cand[:], w=["candl"])
+    dma("S", T.geoi[:], T.geo[:], w=["geoi"])
+    dma("S", T.nbi[:], T.nb[:], w=["nbi"])
+
+    ci, cf = T.ci, T.cf
+
+    def icol(k):
+        return ci[:, k:k + 1]
+
+    def fcol(k):
+        return cf[:, k:k + 1]
+
+    op("G", lambda: g.iota(icol(0), [[0, 1]], 0, 1), w=["ci0"])
+    op("G", lambda: g.iota(T.posc[:], [[1, 8], [448, 4]], 0, 0, allow_small_or_imprecise_dtypes=True), w=["posc"])
+    op("V", ms(T.ones[:], 1.0), w=["ones"])
+    op("V", ms(T.cq[:], 0.0), w=["cq"])
+    op("G", lambda: g.affine_select(T.bt[:], T.ones[:], [[-16, 8], [0, 16]], A.is_ge, 0.0, 0, 1), r=["ones"], w=["bt"])
+    op("G", lambda: g.affine_select(T.bm[:], T.bt[:], [[16, 8], [0, 16]], A.is_ge, 0.0, 15, -1), r=["bt"], w=["bm"])
+    op("G", lambda: g.iota(T.qrow[:], [[0, 8], [1, 16]], 0, 0, allow_small_or_imprecise_dtypes=True), w=["qrow"])
+    op("G", lambda: g.affine_select(T.ip[:], T.ones[:], [[-1, 128]], A.is_equal, 0.0, 0, 1), r=["ones"], w=["ip"])
+    op("G", lambda: g.iota(T.headc[:], [[0, 8], [448, 4]], 8, 0, allow_small_or_imprecise_dtypes=True), w=["headc"])
+    op("G", lambda: g.iota(T.sbase[:], [[0, 8], [-7164, 4]], 0, 0, allow_small_or_imprecise_dtypes=True), w=["sbase"])
+    op("V", ts(icol(1), icol(0), 15, A.bitwise_and), r=["ci0"], w=["ci1"])
+    op("V", cp(fcol(1), icol(1)), r=["ci1"], w=["cf1"])
+    op("V", ts(fcol(2), fcol(1), 28.0, A.mult), r=["cf1"], w=["cf2"])
+    op("V", ts(fcol(3), fcol(1), 1.5, A.is_lt), r=["cf1"], w=["cf3"])
+    op("V", ts(T.posc[:], T.posc[:], fcol(2), A.add), r=["posc", "cf2"], w=["posc"])
+    for c in range(NCH):
+        op("V", cp(T.offc[:, 8 * c:8 * c + 8], T.posc[:, c:32:4]), r=["posc"], w=["offc%d" % c])
+    op("V", ts(T.clo[:], T.candl[:], 63, A.bitwise_and), r=["candl"], w=["clo"])
+    op("V", tt(T.chib[:], T.candl[:], T.clo[:], A.subtract), r=["clo", "candl"], w=["chib"])
+    op("V", cp(T.clob[:], T.clo[:]), r=["clo"], w=["clob"])
+    dma("Y", T.cq[0:128:16, :], T.chib[:], r=["chib", "cq"], w=["cqh"])
+    dma("S", T.cq[1:128:16, :], T.clob[:], r=["clob", "cq"], w=["cql"])
+    dma("Y", T.pw[:], T.pe[:], r=["chib"], w=["pw"])
+    dma("Y", T.sw[:], T.se[:], w=["sw"])
+    op("V", ms(T.csel[:], 0.0), w=["csel"])
+    op("V", ms(T.casel[:], 0.0), w=["casel"])
+    op("V", ts(T.selk[:], T.bm[:], fcol(3), A.mult), r=["bm", "cf3"], w=["selk"])
+    op("V", ts(T.m16[:], T.qrow[:, 0:16], fcol(1), A.is_equal), r=["qrow", "cf1"], w=["m16"])
+    op("V", cp(T.geof[:], T.geoi[:]), r=["geoi"], w=["geof"])
+    op("V", cp(T.bf32[:], T.bm[:]), r=["bm"], w=["bf32"])
+    for u in range(8):
+        op("V", cp(T.csel[:, u, :, u, :], T.selk[:, u:64:8, :]), r=["selk", "csel"], w=["cselu%d" % u])
+    for b in range(2):
+        op("V", cp(T.casel[:, b, :, b], T.selk[:, :, b]), r=["selk", "casel"], w=["caselb%d" % b])
+    GM = []
+    for c in range(NCH):
+        for j in range(4):
+            GM.append("gm%d%d" % (c, j))
+            op("V", ts(T.gm[:, 64 * c + 16 * j:64 * c + 16 * j + 16], T.m16[:], T.geof[:, 4 * j + c:4 * j + c + 1], A.mult), r=["m16", "geof"], w=[GM[-1]])
+    op("P", mm(T.jb[:, 2:4, :, :], T.bf32[:], T.gm[:], True, True), r=["bf32"] + GM, w=["jb"], x=["jb"])
+    for c in range(NCH):
+        for al in range(4):
+            o, i = T.geor[:, 4 * c + al, :, :], T.jb[:, 2 + c // 2, 4 * (c % 2):4 * (c % 2) + 4, :]
+            op("S", lambda o=o, i=i: S.activation(o, i, COPY, bias=-65536.0, scale=16.0), r=["jb"], w=["geor%d" % (4 * c + al)], x=["jb"])
+
+    def gather_codes(c):
+        op("V", cp(T.crow[:, c, :], T.cq[:].indirect(T.offc[:, 8 * c:8 * c + 8])),
+           r=["cq", "cqh", "cql", "offc%d" % c], w=["crow%d" % c])
+
+    ALLC = ["crow%d" % c for c in range(NCH)]
+
+    def crow_of(a):
+        return T.crow[:, :, 16 * a:16 * a + 16]
+
+    def send_codes(t):
+        op("P", [mm(T.mb[:, 1, 64:128], T.csel[:, u, :, :, :], crow_of(u), u == 0, u == 7) for u in range(8)],
+           r=ALLC + ["cselu%d" % u for u in range(8)], w=["mb"], x=["mb"])
+        mine = W[t][:, 64 * rank:64 * rank + 64]
+        op("V", cp(mine, T.mb[:, 1, 64:128]), r=["mb"], w=["wown%d" % t], x=["mb"])
+        need("G", deps("G", ["wown%d" % t], [], []))
+        m = topo.mask(core, others[0])
+        ids = []
+        for o in others:
+            m &= topo.mask(core, o)
+            a = topo.addr(o)
+            ids.append(DstId(rid=a[0], pnc=a[1]))
+        tr = RemoteDMATransfer(dst_ids=ids, dma_engine_mask=m, remote_sem=T.sem["arr%d" % t], srcs=[mine], dsts=[mine for _ in ids])
+        g.remote_dma_fused([tr], local_sem=T.sem.loc)
+        return bin(m).count("1")
+
+    def own_codes(t):
+        for al in range(4):
+            calls = []
+            for j in range(4):
+                for b in range(2):
+                    calls.append(mm(CA[al // 2][:, al % 2, j, :], T.casel[:, b, :, :], crow_of(slot(t, al, b)), b == 0, b == 1))
+            op("P", calls, r=ALLC + ["caselb0", "caselb1"], w=["ca%d" % al], x=["cab%d" % (al // 2)])
+
+    def self_list():
+        op("V", ts(T.sbf[:], T.posc[:], 16.0, A.mult), r=["posc"], w=["sbf"])
+        op("V", tt(T.sbf[:], T.sbf[:], T.sbase[:], A.add), r=["sbf", "sbase"], w=["sbf"])
+        op("V", cp(T.offs[:], T.sbf[:]), r=["sbf"], w=["offs"])
+
+    def self_gather():
+        op("S", lambda: S.activation(T.own[:], T.sq[:].indirect(T.offs[:]), COPY), r=["sq", "offs"], w=["own"])
+
+    def self_gaps(t):
+        for k in range(8):
+            a = slot(t, k // 2, k % 2)
+            b = (a + 1 + t) % 8
+            op("V", tt(T.ns[:, :, k, :], T.own[:, 64 * b:64 * b + 64], T.own[:, 64 * a:64 * a + 64], A.subtract), r=["own"], w=["ns%d" % k])
+
+    NS = ["ns%d" % k for k in range(8)]
+
+    def code_rows(t):
+        op("P", [mm(T.mb[:], T.selk[:], T.crow[:], True, True)], r=ALLC + ["selk"], w=["mb"], x=["mb"])
+        for k in range(8):
+            a = slot(t, k // 2, k % 2)
+            op("V", cp(T.cr[:, :, k, :], T.mb[:, :, 16 * a:16 * a + 16]), r=["mb"], w=["cr%d" % k], x=["mb"])
+
+    def neighbours(t, c0, c1):
+        op("V", cp(T.cn[:, 64 * c0:64 * c1], W[t][:].indirect(T.nbu[:, 4 * c0:4 * c1])), r=["nbu", "wown%d" % t],
+           w=["cn%d" % c for c in range(c0, c1)])
+
+    def index(t, c, split):
+        ks = [4 * c + al for al in range(4)]
+        for al in range(4):
+            ca = CA[al // 2][:, al % 2, :, 16 * c:16 * c + 16]
+            op("V", tt(ca, T.cn[:, 64 * c:64 * c + 64], ca, A.mult), r=["cn%d" % c, "ca%d" % al], w=["pr%d" % ks[al]], x=["cab%d" % (al // 2)])
+        for al in range(4):
+            ca = CA[al // 2][:, al % 2, :, 16 * c:16 * c + 16]
+            op("V", tt(T.idx[:, ks[al], :, :], ca, T.geor[:, ks[al], :, :], A.add), r=["pr%d" % ks[al], "geor%d" % ks[al]], w=["ix%d" % ks[al]], x=["cab%d" % (al // 2)])
+        groups = [[k] for k in ks] if split else [ks]
+        for gr in groups:
+            v = T.idx[:, gr[0]:gr[-1] + 1, :, :]
+            op("V", ts(v, v, 4, A.arith_shift_right, 4095, A.bitwise_and), r=["ix%d" % k for k in gr], w=["ix%d" % k for k in gr])
+        for gr in groups:
+            op("V", cp(T.off[:, 64 * gr[0]:64 * gr[-1] + 64], T.idx[:, gr[0]:gr[-1] + 1, :, :]), r=["ix%d" % k for k in gr], w=["of%d" % k for k in gr])
+
+    def gather(c, al, hs):
+        k = 4 * c + al
+        lo, n = 64 * k + 32 * hs[0], 32 * len(hs)
+        op("S", lambda: S.activation(E[c][:, 16 * lo - 4096 * c:16 * (lo + n) - 4096 * c], T.pw[:].indirect(T.off[:, lo:lo + n]), COPY),
+           r=["pw", "of%d" % k], w=["e%d%d%d" % (c, al, h) for h in hs])
+
+    nd = [0]
+
+    def pe_diff(c, h, plus, minus, flip=False):
+        i = nd[0] % 4
+        nd[0] += 1
+        calls = []
+        for j in range(2):
+            for b in range(2):
+                o = D[i][:, 256 * j + 128 * b:256 * j + 128 * b + 128]
+                p, q = [1024 * al + 512 * h + 256 * j for al in (plus, minus)]
+                b2 = 1 - b if flip else b
+                calls.append(mm(o, T.ip[:], E[c][:, p + b:p + 256:2], True, False))
+                calls.append(mm(o, T.im[:], E[c][:, q + b2:q + 256:2], False, True))
+        op("P", calls, r=["e%d%d%d" % (c, plus, h), "e%d%d%d" % (c, minus, h), "ip", "im"], w=["d%d" % i], x=["d%d" % i])
+        return (D[i], "d%d" % i, True)
+
+    def fused(c, h, other, out, key):
+        k = 4 * c + 1
+        lo = 64 * k + 32 * h
+        p = 1024 * other + 512 * h
+        op("V", tt(out[:], T.pw[:].indirect(T.off[:, lo:lo + 32]), E[c][:, p:p + 512], A.subtract), r=["pw", "of%d" % k, "e%d%d%d" % (c, other, h)], w=[key])
+        return (out, key, False)
+
+    def scan(c, al, h, src, low):
+        rp = T.rmin if low else T.rmax
+        o0, o1 = (A.max, A.min) if low else (A.min, A.max)
+        k = 4 * h + al
+        if src[2]:
+            calls = [lambda: V.tensor_tensor_scan(SC[c][:, k, :], rp[:], src[0][:], 0.0, o0, o1)]
+        else:
+            calls = [lambda j=j, b=b: V.tensor_tensor_scan(SC[c][:, k, 256 * j + 128 * b:256 * j + 128 * b + 128], rp[:, 0:128],
+                                                           src[0][:, 256 * j + b:256 * j + 256:2], 0.0, o0, o1) for j in range(2) for b in range(2)]
+        op("V", calls, r=[src[1], "rmin" if low else "rmax"], w=["sc%d%d%d" % (c, al, h)], x=[src[1]] if src[2] else [])
+
+    def jsum(t, c):
+        sets = [(0, 1, False), (1, 4, True)] if t < 3 else [(0, 2, True), (2, 4, False)]
+        calls = []
+        for a0, a1, pos in sets:
+            for j in range(4):
+                h, lo = 4 * (j // 2), 256 * (j % 2)
+                calls.append(mm(T.jb[:, 0, 2 * a0:2 * a1, :], (T.ip if pos else T.im)[:], SC[c][:, h + a0:h + a1, lo + 7:lo + 256:8], j == 0, j == 3))
+        op("P", calls, r=["ip", "im"] + ["sc%d%d%d" % (c, al, h) for al in range(4) for h in range(2)], w=["jb"], x=["jb"])
+
+    def flag(c):
+        op("V", tt(T.flg[:], T.jb[:, 0, :, :], T.ns[:, c, :, :], A.is_gt), r=["jb"] + NS, w=["flg"], x=["jb"])
+
+    def post(t, c):
+        def s0():
+            jsum(t, c)
+
+        def s1():
+            flag(c)
+            if t == 3:
+                for k in range(8):
+                    op("V", tt(T.ygb[:, 16 * c:16 * c + 16, slot(t, k // 2, k % 2)], T.jb[:, 0, k, :], T.ns[:, c, k, :], A.subtract), r=["jb"] + NS, w=["yg%d%d" % (c, k)], x=["jb"])
+
+        def s2():
+            if t < 3:
+                op("P", mm(T.mb[:, 0, :], T.flg[:], T.bm[:], True, True), r=["flg", "bm"], w=["mb"], x=["mb"])
+            else:
+                op("P", [mm(T.mb[:, 0, :], T.kc[:], T.ones[:], True, False), mm(T.mb[:, 0, :], T.bn[:], T.flg[:], False, True)],
+                   r=["flg", "bn", "kc", "ones"], w=["mb"], x=["mb"])
+
+        def s3():
+            if t < 3:
+                op("V", tt(T.dm[:], T.mb[:, 0, :], T.thr[:], A.is_ge), r=["mb", "thr"], w=["dm"], x=["mb"])
+            else:
+                for k in range(8):
+                    op("V", tt(T.ycb[:, 16 * c:16 * c + 16, slot(t, k // 2, k % 2)], T.mb[:, 0, 16 * k:16 * k + 16], T.cr[:, c, k, :], A.min), r=["mb", "cr%d" % k], w=["yc%d%d" % (c, k)], x=["mb"])
+
+        def s4():
+            if t < 3:
+                op("P", mm(T.mb[:, 1, 0:24], T.dm[:], RT[t][:], True, True), r=["dm", "rt%d" % t], w=["mb"], x=["mb"])
+
+        def s5():
+            if t < 3:
+                p, h = T.posc[:, c:32:4], T.headc[:, c:32:4]
+                op("V", tt(T.t1[:], T.mb[:, 1, 0:8], p, A.add), r=["mb", "posc"], w=["t1"], x=["mb"])
+                op("V", tt(T.t3[:], T.mb[:, 1, 8:16], h, A.add), r=["mb", "headc"], w=["t3"], x=["mb"])
+                op("V", tt(p, T.t1[:], T.t3[:], A.min), r=["t1", "t3"], w=["posc"])
+                op("V", cp(T.offc[:, 8 * c:8 * c + 8], p), r=["posc"], w=["offc%d" % c])
+                op("V", tt(h, T.mb[:, 1, 16:24], h, A.add), r=["mb", "headc"], w=["headc"], x=["mb"])
+                gather_codes(c)
+        return [s0, s1, s2, s3, s4, s5]
+
+    nsig = []
+    for c in range(NCH):
+        gather_codes(c)
+    nsig.append(send_codes(0))
+    own_codes(0)
+
+    for j in range(4):
+        op("V", cp(T.nbu[:, j:16:4], T.nbi[:, 4 * j:4 * j + 4]), r=["nbi"], w=["nbu"])
+    op("V", ts(icol(3), icol(0), 5, A.arith_shift_right), r=["ci0"], w=["ci3"])
+    op("V", ts(icol(4), icol(0), 4, A.arith_shift_right, 1, A.bitwise_and), r=["ci0"], w=["ci4"])
+    op("V", ts(icol(5), icol(1), 3, A.bitwise_and), r=["ci1"], w=["ci5"])
+    op("V", ts(icol(6), icol(1), 2, A.arith_shift_right), r=["ci1"], w=["ci6"])
+    op("V", cp(fcol(0), icol(0)), r=["ci0"], w=["cf0"])
+    for k in (3, 4, 5, 6):
+        op("V", cp(fcol(k + 2), icol(k)), r=["ci%d" % k], w=["cf%d" % (k + 2)])
+    op("V", ms(T.rmin[:], -BIG), w=["rmin"])
+    op("V", ms(T.rmax[:], BIG), w=["rmax"])
+    op("V", ts(T.im[:], T.ip[:], -1.0, A.mult), r=["ip"], w=["im"])
+    op("V", ts(fcol(9), fcol(6), 4.0, A.mult), r=["cf6"], w=["cf9"])
+    op("V", ts(fcol(11), fcol(5), 2.0, A.mult), r=["cf5"], w=["cf11"])
+    op("V", ts(fcol(12), fcol(5), 3.0, A.mult), r=["cf5"], w=["cf12"])
+    op("V", ms(T.rmin[:, 0:512:8], BIG), w=["rmin"])
+    op("V", ms(T.rmax[:, 0:512:8], -BIG), w=["rmax"])
+    op("V", ts(T.headc[:], T.headc[:], fcol(2), A.add), r=["headc", "cf2"], w=["headc"])
+    op("V", tt(fcol(10), fcol(9), fcol(5), A.add), r=["cf9", "cf5"], w=["cf10"])
+    op("V", tt(fcol(11), fcol(11), fcol(6), A.add), r=["cf11", "cf6"], w=["cf11"])
+    op("V", tt(icol(7), fcol(12), fcol(9), A.add), r=["cf12", "cf9"], w=["ci7"])
+    op("V", ts(icol(8), icol(7), 7, A.bitwise_and), r=["ci7"], w=["ci8"])
+    op("V", cp(fcol(12), icol(8)), r=["ci8"], w=["cf12"])
+    for t in range(3):
+        a = fcol(10 + t)
+        k = "cf%d" % (10 + t)
+        op("V", ts(RT[t][:, 0:8], T.qrow[:, 0:8], a, A.is_equal, 4096.0, A.mult), r=["qrow", k], w=["rta%d" % t])
+        op("V", ts(RT[t][:, 8:16], T.qrow[:, 0:8], a, A.is_gt), r=["qrow", k], w=["rtb%d" % t])
+        op("V", ms(RT[t][:, 16:24], 1.0), r=["rta%d" % t, "rtb%d" % t], w=["rt%d" % t])
+    op("V", ts(T.thr[:], T.qrow[:], fcol(1), A.not_equal, 1000.0, A.mult), r=["qrow", "cf1"], w=["thr"])
+    op("V", ts(fcol(13), fcol(7), 448.0, A.mult), r=["cf7"], w=["cf13"])
+    op("V", ts(fcol(14), fcol(1), -448.0, A.mult), r=["cf1"], w=["cf14"])
+    op("V", ts(T.thr[:], T.thr[:], 15.5, A.max), r=["thr"], w=["thr"])
+    op("V", tt(fcol(13), fcol(13), fcol(8), A.add), r=["cf13", "cf8"], w=["cf13"])
+    op("V", cp(T.cand16[:], T.candl[:]), r=["candl"], w=["cand16"])
+    op("V", tt(fcol(13), fcol(13), fcol(14), A.add), r=["cf13", "cf14"], w=["cf13"])
+    op("V", ts(T.sbase[:], T.sbase[:], fcol(13), A.add), r=["sbase", "cf13"], w=["sbase"])
+
+    def last_constants():
+        op("V", ts(T.bn[:], T.bm[:], -4096.0, A.mult), r=["bm"], w=["bn"])
+        op("V", ts(fcol(14), fcol(0), 0.0, A.is_equal, 65536.0, A.mult), r=["cf0"], w=["cf14"])
+        op("V", ts(fcol(15), fcol(0), 1.0, A.is_equal), r=["cf0"], w=["cf15"])
+        op("V", tt(fcol(14), fcol(14), fcol(15), A.subtract), r=["cf14", "cf15"], w=["cf14"])
+        op("V", ts(T.kc[:], T.ones[:], fcol(14), A.mult), r=["ones", "cf14"], w=["kc"])
+
+    for t in range(4):
+        V.wait_ge(T.sem["arr%d" % t], 3 * nsig[t])
+        neighbours(t, 0, 1)
+        index(t, 0, True)
+        neighbours(t, 1, NCH)
+        for c in range(NCH):
+            stages = post(t, c - 1) if c else [lambda: None] * 6
+            order = [(0, [0, 1]), (1, [1]), (2, [0, 1]), (3, [0, 1])] if t < 3 else [(3, [0, 1]), (1, [1]), (0, [0, 1]), (2, [0, 1])]
+            for al, hs in order[:3]:
+                gather(c, al, hs)
+            if t == 0 and c == 1:
+                op("V", cp(T.sq[:], T.sw[:].indirect(T.cand16[:])), r=["sw", "cand16"], w=["sq"])
+                self_list()
+                self_gather()
+                self_gaps(t)
+            last = order[3][0]
+            if c < NCH - 1:
+                gather(c, last, [0, 1])
+            else:
+                gather(c, last, [0])
+                gather(c, last, [1])
+            if c + 1 < NCH:
+                index(t, c + 1, False)
+            if t < 3:
+                flip = (t != 1)
+                b0 = pe_diff(c, 1, 1, 0)
+                f0 = fused(c, 0, 0, T.fa, "fa")
+                stages[0]()
+                scan(c, 0, 0, f0, False)
+                stages[1]()
+                b1 = pe_diff(c, 1, 1, 2)
+                stages[2]()
+                scan(c, 0, 1, b0, False)
+                stages[3]()
+                f1 = fused(c, 0, 2, T.fb, "fb")
+                stages[4]()
+                b2 = pe_diff(c, 0, 2, 3)
+                scan(c, 1, 0, f1, True)
+                scan(c, 1, 1, b1, True)
+                stages[5]()
+                b3 = pe_diff(c, 0, 3, 0, flip)
+                scan(c, 2, 0, b2, True)
+                b4 = pe_diff(c, 1, 2, 3)
+                scan(c, 3, 0, b3, True)
+                b5 = pe_diff(c, 1, 3, 0, flip)
+                scan(c, 2, 1, b4, True)
+                scan(c, 3, 1, b5, True)
+            else:
+                b0 = pe_diff(c, 1, 1, 3)
+                f0 = fused(c, 0, 3, T.fa, "fa")
+                stages[0]()
+                scan(c, 1, 0, f0, True)
+                scan(c, 3, 0, f0, False)
+                stages[1]()
+                stages[2]()
+                scan(c, 1, 1, b0, True)
+                scan(c, 3, 1, b0, False)
+                stages[3]()
+                b1 = pe_diff(c, 0, 0, 2)
+                b2 = pe_diff(c, 1, 0, 2)
+                scan(c, 0, 0, b1, True)
+                scan(c, 2, 0, b1, False)
+                scan(c, 0, 1, b2, True)
+                scan(c, 2, 1, b2, False)
+                if c == 3:
+                    dma("Y", T.yg[:, 0:384], T.ygb[:, 0:48, :], r=["yg%d%d" % (i, k) for i in range(3) for k in range(8)])
+                    dma("Y", T.yc[:, 0:384], T.ycb[0:128:16, 0:48, :], r=["yc%d%d" % (i, k) for i in range(3) for k in range(8)])
+        for st in post(t, NCH - 1):
+            st()
+        if t < 3:
+            nsig.append(send_codes(t + 1))
+            own_codes(t + 1)
+            self_list()
+            self_gather()
+            self_gaps(t + 1)
+            if t == 2:
+                code_rows(3)
+                last_constants()
+    dma("Y", T.yg[:, 384:512], T.ygb[:, 48:64, :], r=["yg3%d" % k for k in range(8)])
+    dma("S", T.yc[:, 384:512], T.ycb[0:128:16, 48:64, :], r=["yc3%d" % k for k in range(8)])
+    g.wait_ge(T.sem.loc, sum(nsig))
+    for e in ("sV", "sS", "sP", "sG"):
+        if know["Y"].get(e, 0) < count[e]:
+            g.sync.wait_ge(T.sem[e], count[e])
+    for i in range(ndma[0]):
+        g.sync.wait_ge(T.sem["dma%d" % i], 16)

@@ -4,6 +4,10 @@ from concourse.mybir import AluOpType, ActivationFunctionType
 BF, F32, I32, U16 = "bfloat16", "float32", "int32", "uint16"
 NCH = 4
 BIG = 1024.0
+STYLE = [[0, 1, 1, 0], [1, 1, 1, 0], [1, 1, 1, 0], [1, 1, 0, 0]]
+VG = [[0, 1], [0, 1], [0], []]
+AHEAD = [[1, 2], [3], [], []]
+SPLIT = 1024
 SCRATCH = {
     "pw": ("sbuf", [128, 4096], BF), "sw": ("sbuf", [128, 4096], I32), "sq": ("sbuf", [128, 1792], F32),
     "cq": ("sbuf", [128, 1792], BF),
@@ -25,6 +29,7 @@ SCRATCH = {
     "cn": ("sbuf", [128, 256], F32), "idx": ("sbuf", [128, 16, 4, 16], I32), "off": ("sbuf", [128, 1024], U16),
     "flg": ("sbuf", [128, 128], BF), "dm": ("sbuf", [128, 128], BF),
     "ygb": ("sbuf", [128, 64, 8], F32), "ycb": ("sbuf", [128, 64, 8], F32),
+    "n0": ("sbuf", [128, 512], BF), "n1": ("sbuf", [128, 512], BF), "n2": ("sbuf", [128, 512], BF),
     "fa": ("sbuf", [128, 512], BF), "fb": ("sbuf", [128, 512], BF),
     "d0": ("psum", [128, 512], F32), "d1": ("psum", [128, 512], F32), "d2": ("psum", [128, 512], F32), "d3": ("psum", [128, 512], F32),
     "ca0": ("psum", [128, 2, 4, 64], F32), "ca1": ("psum", [128, 2, 4, 64], F32),
@@ -34,7 +39,7 @@ for _c in range(NCH):
     SCRATCH["e%d" % _c] = ("sbuf", [128, 4096], BF)
     SCRATCH["sc%d" % _c] = ("sbuf", [128, 8, 512], BF)
 NDMA = 12
-SEMAPHORES = ["sV", "sS", "sP", "sG", "loc"] + ["arr%d" % i for i in range(4)] + ["dma%d" % i for i in range(NDMA)]
+SEMAPHORES = ["sV", "sS", "sP", "sG", "loc"] + ["arr%d" % i for i in range(4)] + ["dma%d" % i for i in range(NDMA)] + ["add%d" % i for i in range(8)]
 
 
 def slot(t, al, b):
@@ -101,28 +106,34 @@ def rank_program(g, core, T, topo):
         for k in x:
             bank.setdefault(k, {})[tok[0]] = tok
 
+    def done(e, sem, val, r, w, x=()):
+        sn = dict(know[e])
+        sn[sem] = val
+        snaps[(sem, val)] = sn
+        mark((sem, val), r, w, x)
+
     def op(e, calls, r=(), w=(), x=()):
         need(e, deps(e, r, w, x))
         sem = "s" + e
         for call in (calls if isinstance(calls, list) else [calls]):
             call().then_inc(T.sem[sem], 1)
             count[sem] += 1
-        tok = (sem, count[sem])
-        sn = dict(know[e])
-        sn[sem] = count[sem]
-        snaps[tok] = sn
-        mark(tok, r, w, x)
+        done(e, sem, count[sem], r, w, x)
 
     def dma(e, out, in_, r=(), w=()):
         need(e, deps("dma", r, w, ()))
         sem = "dma%d" % ndma[0]
         ndma[0] += 1
         queue[e].dma_start(out, in_).then_inc(T.sem[sem], 16)
-        tok = (sem, 16)
-        sn = dict(know[e])
-        sn[sem] = 16
-        snaps[tok] = sn
-        mark(tok, r, w, ())
+        done(e, sem, 16, r, w)
+
+    nadd = [0] * 8
+
+    def dma_add(i, out, in_, r, w):
+        need("G", deps("dma", r, w, ()))
+        nadd[i] += 16
+        g.dma_start(out, in_, accum_op=A.add).then_inc(T.sem["add%d" % i], 16)
+        done("G", "add%d" % i, nadd[i], r, w)
 
     W = [T.w0, T.w1, T.w2, T.w3]
     D = [T.d0, T.d1, T.d2, T.d3]
@@ -150,6 +161,7 @@ def rank_program(g, core, T, topo):
         return lambda: P.matmul(out, l, rhs, st, sp)
 
     dma("Y", T.candl[:], T.cand[:], w=["candl"])
+    dma("Y", T.pw[:, 0:SPLIT], T.pe[:, 0:SPLIT], w=["pwa"])
     dma("S", T.geoi[:], T.geo[:], w=["geoi"])
     dma("S", T.nbi[:], T.nb[:], w=["nbi"])
 
@@ -176,14 +188,12 @@ def rank_program(g, core, T, topo):
     op("V", ts(fcol(2), fcol(1), 28.0, A.mult), r=["cf1"], w=["cf2"])
     op("V", ts(fcol(3), fcol(1), 1.5, A.is_lt), r=["cf1"], w=["cf3"])
     op("V", ts(T.posc[:], T.posc[:], fcol(2), A.add), r=["posc", "cf2"], w=["posc"])
-    for c in range(NCH):
-        op("V", cp(T.offc[:, 8 * c:8 * c + 8], T.posc[:, c:32:4]), r=["posc"], w=["offc%d" % c])
     op("V", ts(T.clo[:], T.candl[:], 63, A.bitwise_and), r=["candl"], w=["clo"])
     op("V", tt(T.chib[:], T.candl[:], T.clo[:], A.subtract), r=["clo", "candl"], w=["chib"])
     op("V", cp(T.clob[:], T.clo[:]), r=["clo"], w=["clob"])
     dma("Y", T.cq[0:128:16, :], T.chib[:], r=["chib", "cq"], w=["cqh"])
-    dma("S", T.cq[1:128:16, :], T.clob[:], r=["clob", "cq"], w=["cql"])
-    dma("Y", T.pw[:], T.pe[:], r=["chib"], w=["pw"])
+    dma("Y", T.cq[1:128:16, :], T.clob[:], r=["clob", "cq"], w=["cql"])
+    dma("Y", T.pw[:, SPLIT:4096], T.pe[:, SPLIT:4096], w=["pw"])
     dma("Y", T.sw[:], T.se[:], w=["sw"])
     op("V", ms(T.csel[:], 0.0), w=["csel"])
     op("V", ms(T.casel[:], 0.0), w=["casel"])
@@ -212,15 +222,21 @@ def rank_program(g, core, T, topo):
 
     ALLC = ["crow%d" % c for c in range(NCH)]
 
-    def crow_of(a):
-        return T.crow[:, :, 16 * a:16 * a + 16]
+    def crow_of(a, t, c0=0, c1=NCH):
+        return T.crow[:, c0:c1, 16 * a:16 * a + 16] if t else T.cq[:, a:1792:28]
 
-    def send_codes(t):
-        op("P", [mm(T.mb[:, 1, 64:128], T.csel[:, u, :, :, :], crow_of(u), u == 0, u == 7) for u in range(8)],
-           r=ALLC + ["cselu%d" % u for u in range(8)], w=["mb"], x=["mb"])
-        mine = W[t][:, 64 * rank:64 * rank + 64]
-        op("V", cp(mine, T.mb[:, 1, 64:128]), r=["mb"], w=["wown%d" % t], x=["mb"])
-        need("G", deps("G", ["wown%d" % t], [], []))
+    def crow_keys(t, c0=0, c1=NCH):
+        return ALLC[c0:c1] if t else ["cq", "cqh", "cql"]
+
+    def code_sums(t, c0, c1):
+        op("P", [mm(T.mb[:, 1, 64 + 16 * c0:64 + 16 * c1], T.csel[:, u, :, :, :], crow_of(u, t, c0, c1), u == 0, u == 7) for u in range(8)],
+           r=crow_keys(t, c0, c1) + ["cselu%d" % u for u in range(8)], w=["mb"], x=["mb"])
+
+    def send_codes(t, c0, c1):
+        mine = W[t][:, 64 * rank + 16 * c0:64 * rank + 16 * c1]
+        key = "wown%d%d" % (t, c0)
+        op("V", cp(mine, T.mb[:, 1, 64 + 16 * c0:64 + 16 * c1]), r=["mb"], w=[key], x=["mb"])
+        need("G", deps("G", [key], [], []))
         m = topo.mask(core, others[0])
         ids = []
         for o in others:
@@ -236,8 +252,8 @@ def rank_program(g, core, T, topo):
             calls = []
             for j in range(4):
                 for b in range(2):
-                    calls.append(mm(CA[al // 2][:, al % 2, j, :], T.casel[:, b, :, :], crow_of(slot(t, al, b)), b == 0, b == 1))
-            op("P", calls, r=ALLC + ["caselb0", "caselb1"], w=["ca%d" % al], x=["cab%d" % (al // 2)])
+                    calls.append(mm(CA[al // 2][:, al % 2, j, :], T.casel[:, b, :, :], crow_of(slot(t, al, b), t), b == 0, b == 1))
+            op("P", calls, r=crow_keys(t) + ["caselb0", "caselb1"], w=["ca%d" % al], x=["cab%d" % (al // 2)])
 
     def self_list():
         op("V", ts(T.sbf[:], T.posc[:], 16.0, A.mult), r=["posc"], w=["sbf"])
@@ -262,52 +278,87 @@ def rank_program(g, core, T, topo):
             op("V", cp(T.cr[:, :, k, :], T.mb[:, :, 16 * a:16 * a + 16]), r=["mb"], w=["cr%d" % k], x=["mb"])
 
     def neighbours(t, c0, c1):
-        op("V", cp(T.cn[:, 64 * c0:64 * c1], W[t][:].indirect(T.nbu[:, 4 * c0:4 * c1])), r=["nbu", "wown%d" % t],
+        op("V", cp(T.cn[:, 64 * c0:64 * c1], W[t][:].indirect(T.nbu[:, 4 * c0:4 * c1])), r=["nbu", "wown%d0" % t, "wown%d3" % t],
            w=["cn%d" % c for c in range(c0, c1)])
 
-    def index(t, c, split):
-        ks = [4 * c + al for al in range(4)]
-        for al in range(4):
+    def index(c, first=()):
+        def product(al):
             ca = CA[al // 2][:, al % 2, :, 16 * c:16 * c + 16]
-            op("V", tt(ca, T.cn[:, 64 * c:64 * c + 64], ca, A.mult), r=["cn%d" % c, "ca%d" % al], w=["pr%d" % ks[al]], x=["cab%d" % (al // 2)])
-        for al in range(4):
-            ca = CA[al // 2][:, al % 2, :, 16 * c:16 * c + 16]
-            op("V", tt(T.idx[:, ks[al], :, :], ca, T.geor[:, ks[al], :, :], A.add), r=["pr%d" % ks[al], "geor%d" % ks[al]], w=["ix%d" % ks[al]], x=["cab%d" % (al // 2)])
-        groups = [[k] for k in ks] if split else [ks]
-        for gr in groups:
-            v = T.idx[:, gr[0]:gr[-1] + 1, :, :]
-            op("V", ts(v, v, 4, A.arith_shift_right, 4095, A.bitwise_and), r=["ix%d" % k for k in gr], w=["ix%d" % k for k in gr])
-        for gr in groups:
-            op("V", cp(T.off[:, 64 * gr[0]:64 * gr[-1] + 64], T.idx[:, gr[0]:gr[-1] + 1, :, :]), r=["ix%d" % k for k in gr], w=["of%d" % k for k in gr])
+            op("V", tt(ca, T.cn[:, 64 * c:64 * c + 64], ca, A.mult), r=["cn%d" % c, "ca%d" % al], w=["pr%d" % (4 * c + al)], x=["cab%d" % (al // 2)])
 
-    def gather(c, al, hs):
+        def shift(al):
+            k = 4 * c + al
+            ca = CA[al // 2][:, al % 2, :, 16 * c:16 * c + 16]
+            op("V", tt(T.idx[:, k, :, :], ca, T.geor[:, k, :, :], A.add), r=["pr%d" % k, "geor%d" % k], w=["ix%d" % k], x=["cab%d" % (al // 2)])
+
+        def wrap(ks):
+            v = T.idx[:, ks[0]:ks[-1] + 1, :, :]
+            op("V", ts(v, v, 4, A.arith_shift_right, 4095, A.bitwise_and), r=["ix%d" % k for k in ks], w=["ix%d" % k for k in ks])
+
+        def narrow(ks):
+            op("V", cp(T.off[:, 64 * ks[0]:64 * ks[-1] + 64], T.idx[:, ks[0]:ks[-1] + 1, :, :]), r=["ix%d" % k for k in ks], w=["of%d" % k for k in ks])
+
+        if not first:
+            ks = [4 * c + al for al in range(4)]
+            for al in range(4):
+                product(al)
+            for al in range(4):
+                shift(al)
+            wrap(ks)
+            narrow(ks)
+        else:
+            for als in ([first[0]], first[1:]):
+                for al in als:
+                    product(al)
+                for al in als:
+                    shift(al)
+                for al in als:
+                    wrap([4 * c + al])
+                for al in als:
+                    narrow([4 * c + al])
+
+    def gather(c, al, hs, sign=1.0, e="S"):
         k = 4 * c + al
         lo, n = 64 * k + 32 * hs[0], 32 * len(hs)
-        op("S", lambda: S.activation(E[c][:, 16 * lo - 4096 * c:16 * (lo + n) - 4096 * c], T.pw[:].indirect(T.off[:, lo:lo + n]), COPY),
-           r=["pw", "of%d" % k], w=["e%d%d%d" % (c, al, h) for h in hs])
+        out, src = E[c][:, 16 * lo - 4096 * c:16 * (lo + n) - 4096 * c], T.pw[:].indirect(T.off[:, lo:lo + n])
+        call = cp(out, src) if e == "V" else (lambda: S.activation(out, src, COPY, scale=sign))
+        op(e, call, r=["pw", "pwa", "of%d" % k], w=["e%d%d%d" % (c, al, h) for h in hs])
+
+    def added(c, i, into, what):
+        p, q = 1024 * into, 1024 * what
+        dma_add(2 * c + i, E[c][:, p:p + 1024], E[c][:, q:q + 1024], ["e%d%d%d" % (c, what, h) for h in range(2)], ["e%d%d%d" % (c, into, h) for h in range(2)])
+
+    def held(c, al, h):
+        return (E[c], "e%d%d%d" % (c, al, h), False, 1024 * al + 512 * h)
 
     nd = [0]
 
-    def pe_diff(c, h, plus, minus, flip=False):
+    def pe_diff(c, h, plus, minus, flip=False, negated=False):
         i = nd[0] % 4
         nd[0] += 1
+        lp, lm = (T.im, T.ip) if negated else (T.ip, T.im)
         calls = []
         for j in range(2):
             for b in range(2):
                 o = D[i][:, 256 * j + 128 * b:256 * j + 128 * b + 128]
                 p, q = [1024 * al + 512 * h + 256 * j for al in (plus, minus)]
                 b2 = 1 - b if flip else b
-                calls.append(mm(o, T.ip[:], E[c][:, p + b:p + 256:2], True, False))
-                calls.append(mm(o, T.im[:], E[c][:, q + b2:q + 256:2], False, True))
+                calls.append(mm(o, lp[:], E[c][:, p + b:p + 256:2], True, False))
+                calls.append(mm(o, lm[:], E[c][:, q + b2:q + 256:2], False, True))
         op("P", calls, r=["e%d%d%d" % (c, plus, h), "e%d%d%d" % (c, minus, h), "ip", "im"], w=["d%d" % i], x=["d%d" % i])
-        return (D[i], "d%d" % i, True)
+        return (D[i], "d%d" % i, True, 0)
+
+    def narrowed(i, src):
+        out = T["n%d" % i]
+        op("S", lambda: S.activation(out[:], src[0][:], COPY), r=[src[1]], w=["n%d" % i], x=[src[1]])
+        return (out, "n%d" % i, 2, 0)
 
     def fused(c, h, other, out, key):
         k = 4 * c + 1
         lo = 64 * k + 32 * h
         p = 1024 * other + 512 * h
-        op("V", tt(out[:], T.pw[:].indirect(T.off[:, lo:lo + 32]), E[c][:, p:p + 512], A.subtract), r=["pw", "of%d" % k, "e%d%d%d" % (c, other, h)], w=[key])
-        return (out, key, False)
+        op("V", tt(out[:], T.pw[:].indirect(T.off[:, lo:lo + 32]), E[c][:, p:p + 512], A.subtract), r=["pw", "pwa", "of%d" % k, "e%d%d%d" % (c, other, h)], w=[key])
+        return (out, key, False, 0)
 
     def scan(c, al, h, src, low):
         rp = T.rmin if low else T.rmax
@@ -317,8 +368,18 @@ def rank_program(g, core, T, topo):
             calls = [lambda: V.tensor_tensor_scan(SC[c][:, k, :], rp[:], src[0][:], 0.0, o0, o1)]
         else:
             calls = [lambda j=j, b=b: V.tensor_tensor_scan(SC[c][:, k, 256 * j + 128 * b:256 * j + 128 * b + 128], rp[:, 0:128],
-                                                           src[0][:, 256 * j + b:256 * j + 256:2], 0.0, o0, o1) for j in range(2) for b in range(2)]
-        op("V", calls, r=[src[1], "rmin" if low else "rmax"], w=["sc%d%d%d" % (c, al, h)], x=[src[1]] if src[2] else [])
+                                                           src[0][:, src[3] + 256 * j + b:src[3] + 256 * j + 256:2], 0.0, o0, o1) for j in range(2) for b in range(2)]
+        op("V", calls, r=[src[1], "rmin" if low else "rmax"], w=["sc%d%d%d" % (c, al, h)], x=[src[1]] if src[2] is True else [])
+
+    def sums(t, c):
+        for h in range(2):
+            if t < 3:
+                scan(c, 0, h, held(c, 1, h), False)
+                scan(c, 2, h, held(c, 2, h), True)
+            else:
+                for al in range(2):
+                    scan(c, al, h, held(c, al, h), True)
+                    scan(c, al + 2, h, held(c, al, h), False)
 
     def jsum(t, c):
         sets = [(0, 1, False), (1, 4, True)] if t < 3 else [(0, 2, True), (2, 4, False)]
@@ -329,15 +390,12 @@ def rank_program(g, core, T, topo):
                 calls.append(mm(T.jb[:, 0, 2 * a0:2 * a1, :], (T.ip if pos else T.im)[:], SC[c][:, h + a0:h + a1, lo + 7:lo + 256:8], j == 0, j == 3))
         op("P", calls, r=["ip", "im"] + ["sc%d%d%d" % (c, al, h) for al in range(4) for h in range(2)], w=["jb"], x=["jb"])
 
-    def flag(c):
-        op("V", tt(T.flg[:], T.jb[:, 0, :, :], T.ns[:, c, :, :], A.is_gt), r=["jb"] + NS, w=["flg"], x=["jb"])
-
     def post(t, c):
         def s0():
             jsum(t, c)
 
         def s1():
-            flag(c)
+            op("V", tt(T.flg[:], T.jb[:, 0, :, :], T.ns[:, c, :, :], A.is_gt), r=["jb"] + NS, w=["flg"], x=["jb"])
             if t == 3:
                 for k in range(8):
                     op("V", tt(T.ygb[:, 16 * c:16 * c + 16, slot(t, k // 2, k % 2)], T.jb[:, 0, k, :], T.ns[:, c, k, :], A.subtract), r=["jb"] + NS, w=["yg%d%d" % (c, k)], x=["jb"])
@@ -367,14 +425,13 @@ def rank_program(g, core, T, topo):
                 op("V", tt(T.t3[:], T.mb[:, 1, 8:16], h, A.add), r=["mb", "headc"], w=["t3"], x=["mb"])
                 op("V", tt(p, T.t1[:], T.t3[:], A.min), r=["t1", "t3"], w=["posc"])
                 op("V", cp(T.offc[:, 8 * c:8 * c + 8], p), r=["posc"], w=["offc%d" % c])
-                op("V", tt(h, T.mb[:, 1, 16:24], h, A.add), r=["mb", "headc"], w=["headc"], x=["mb"])
                 gather_codes(c)
+                op("V", tt(h, T.mb[:, 1, 16:24], h, A.add), r=["mb", "headc"], w=["headc"], x=["mb"])
         return [s0, s1, s2, s3, s4, s5]
 
-    nsig = []
-    for c in range(NCH):
-        gather_codes(c)
-    nsig.append(send_codes(0))
+    nsig = [0] * 4
+    code_sums(0, 0, NCH)
+    nsig[0] += send_codes(0, 0, NCH)
     own_codes(0)
 
     for j in range(4):
@@ -424,75 +481,163 @@ def rank_program(g, core, T, topo):
 
     for t in range(4):
         V.wait_ge(T.sem["arr%d" % t], 3 * nsig[t])
+        flip = (t != 1)
+        style = STYLE[t]
+        vg = [VG[c] if style[c] else [] for c in range(NCH)]
         neighbours(t, 0, 1)
-        index(t, 0, True)
+        index(0, [2, 1, 0, 3])
+        if vg[0]:
+            gather(0, 1, vg[0], 1.0, "V")
         neighbours(t, 1, NCH)
-        for c in range(NCH):
-            stages = post(t, c - 1) if c else [lambda: None] * 6
-            order = [(0, [0, 1]), (1, [1]), (2, [0, 1]), (3, [0, 1])] if t < 3 else [(3, [0, 1]), (1, [1]), (0, [0, 1]), (2, [0, 1])]
-            for al, hs in order[:3]:
-                gather(c, al, hs)
-            if t == 0 and c == 1:
-                op("V", cp(T.sq[:], T.sw[:].indirect(T.cand16[:])), r=["sw", "cand16"], w=["sq"])
-                self_list()
-                self_gather()
-                self_gaps(t)
-            last = order[3][0]
-            if c < NCH - 1:
-                gather(c, last, [0, 1])
+
+        def scalars(c):
+            if style[c]:
+                sg = [h for h in range(2) if h not in vg[c]]
+                neg2 = -1.0 if t == 3 else 1.0
+                seq = [(2, [0, 1], neg2), (1, sg, 1.0), (0, [0, 1], -neg2), (3, [0, 1], -1.0)]
+            elif c == NCH - 1:
+                seq = [(al, [h], 1.0) for h, als in (([1, [1, 0, 2, 3]], [0, [0, 2, 3]]) if t < 3 else ([1, [1, 3, 0, 2]], [0, [3, 0, 2]])) for al in als]
+            elif t < 3:
+                seq = [(0, [0, 1], 1.0), (1, [1], 1.0), (2, [0, 1], 1.0), (3, [0, 1], 1.0)]
             else:
-                gather(c, last, [0])
-                gather(c, last, [1])
-            if c + 1 < NCH:
-                index(t, c + 1, False)
-            if t < 3:
-                flip = (t != 1)
+                seq = [(3, [0, 1], 1.0), (1, [1], 1.0), (0, [0, 1], 1.0), (2, [0, 1], 1.0)]
+            for al, hs, sign in seq:
+                if hs:
+                    gather(c, al, hs, sign)
+
+        def ahead(c):
+            if c == NCH or t == 3:
+                return None
+            scalars(c)
+            if style[c]:
+                return pe_diff(c, 0, 1, 2), pe_diff(c, 1, 1, 2)
+            if c == NCH - 1:
+                return pe_diff(c, 1, 1, 0), pe_diff(c, 1, 1, 2)
+            return None
+
+        first = ahead(0)
+        todo = []
+        for c in range(NCH):
+            last = c == NCH - 1
+            if t == 3:
+                scalars(c)
+            carry, todo = todo, (post(t, c - 1) if c else [])
+            late = t == 0 and c == 1
+            before = [style[c - 1] if c else 0]
+
+            def nxt(n=1, force=False):
+                if late and not force:
+                    return
+                while carry:
+                    carry.pop(0)()
+                if before[0]:
+                    before[0] = 0
+                    sums(t, c - 1)
+                for _ in range(n):
+                    if todo:
+                        todo.pop(0)()
+
+            for c2 in AHEAD[c]:
+                index(c2)
+            if not last and vg[c + 1]:
+                gather(c + 1, 1, vg[c + 1], 1.0, "V")
+
+            if style[c] and t < 3:
+                b0, b1 = first
+                added(c, 0, 1, 0)
+                b2 = pe_diff(c, 0, 3, 0, flip, True)
+                b3 = pe_diff(c, 1, 3, 0, flip, True)
+                added(c, 1, 2, 3)
+                scan(c, 1, 0, b0, True)
+                scan(c, 1, 1, b1, True)
+                nxt()
+                if late:
+                    first = ahead(c + 1)
+                    op("V", cp(T.sq[:], T.sw[:].indirect(T.cand16[:])), r=["sw", "cand16"], w=["sq"])
+                    self_list()
+                    self_gather()
+                scan(c, 3, 0, b2, True)
+                nxt(2)
+                if not late:
+                    first = ahead(c + 1)
+                scan(c, 3, 1, b3, True)
+                nxt(2)
+                if late:
+                    self_gaps(t)
+            elif style[c]:
+                added(c, 0, 0, 2)
+                added(c, 1, 1, 3)
+                nxt(6)
+            elif t < 3 and last:
+                b0, b1 = first
+                b2 = narrowed(0, pe_diff(c, 1, 2, 3))
+                b3 = narrowed(1, pe_diff(c, 1, 3, 0, flip))
+                scan(c, 0, 1, b0, False)
+                scan(c, 1, 1, b1, True)
+                f0 = fused(c, 0, 0, T.fa, "fa")
+                nxt()
+                scan(c, 2, 1, b2, True)
+                nxt(2)
+                scan(c, 3, 1, b3, True)
+                b4 = narrowed(2, pe_diff(c, 0, 2, 3))
+                nxt(2)
+                b5 = pe_diff(c, 0, 3, 0, flip)
+                scan(c, 0, 0, f0, False)
+                f1 = fused(c, 0, 2, T.fb, "fb")
+                nxt()
+                code_sums(t + 1, 0, NCH - 1)
+                scan(c, 1, 0, f1, True)
+                scan(c, 2, 0, b4, True)
+                nsig[t + 1] += send_codes(t + 1, 0, NCH - 1)
+                scan(c, 3, 0, b5, True)
+            elif t < 3:
                 b0 = pe_diff(c, 1, 1, 0)
                 f0 = fused(c, 0, 0, T.fa, "fa")
-                stages[0]()
                 scan(c, 0, 0, f0, False)
-                stages[1]()
                 b1 = pe_diff(c, 1, 1, 2)
-                stages[2]()
-                scan(c, 0, 1, b0, False)
-                stages[3]()
                 f1 = fused(c, 0, 2, T.fb, "fb")
-                stages[4]()
+                nxt()
+                scan(c, 0, 1, b0, False)
+                nxt(2)
                 b2 = pe_diff(c, 0, 2, 3)
-                scan(c, 1, 0, f1, True)
                 scan(c, 1, 1, b1, True)
-                stages[5]()
+                nxt(2)
+                scan(c, 1, 0, f1, True)
                 b3 = pe_diff(c, 0, 3, 0, flip)
                 scan(c, 2, 0, b2, True)
+                nxt()
                 b4 = pe_diff(c, 1, 2, 3)
                 scan(c, 3, 0, b3, True)
                 b5 = pe_diff(c, 1, 3, 0, flip)
                 scan(c, 2, 1, b4, True)
                 scan(c, 3, 1, b5, True)
+                first = ahead(c + 1)
             else:
                 b0 = pe_diff(c, 1, 1, 3)
-                f0 = fused(c, 0, 3, T.fa, "fa")
-                stages[0]()
-                scan(c, 1, 0, f0, True)
-                scan(c, 3, 0, f0, False)
-                stages[1]()
-                stages[2]()
+                b1 = pe_diff(c, 1, 0, 2)
                 scan(c, 1, 1, b0, True)
                 scan(c, 3, 1, b0, False)
-                stages[3]()
-                b1 = pe_diff(c, 0, 0, 2)
-                b2 = pe_diff(c, 1, 0, 2)
-                scan(c, 0, 0, b1, True)
-                scan(c, 2, 0, b1, False)
-                scan(c, 0, 1, b2, True)
-                scan(c, 2, 1, b2, False)
-                if c == 3:
+                nxt()
+                scan(c, 0, 1, b1, True)
+                scan(c, 2, 1, b1, False)
+                nxt(2)
+                f0 = fused(c, 0, 3, T.fa, "fa")
+                nxt(3)
+                scan(c, 1, 0, f0, True)
+                scan(c, 3, 0, f0, False)
+                b2 = pe_diff(c, 0, 0, 2)
+                scan(c, 0, 0, b2, True)
+                scan(c, 2, 0, b2, False)
+                if last:
                     dma("Y", T.yg[:, 0:384], T.ygb[:, 0:48, :], r=["yg%d%d" % (i, k) for i in range(3) for k in range(8)])
                     dma("Y", T.yc[:, 0:384], T.ycb[0:128:16, 0:48, :], r=["yc%d%d" % (i, k) for i in range(3) for k in range(8)])
+            if late or last or not style[c]:
+                nxt(6, True)
         for st in post(t, NCH - 1):
             st()
         if t < 3:
-            nsig.append(send_codes(t + 1))
+            code_sums(t + 1, NCH - 1, NCH)
+            nsig[t + 1] += send_codes(t + 1, NCH - 1, NCH)
             own_codes(t + 1)
             self_list()
             self_gather()

@@ -4,10 +4,20 @@ from concourse.mybir import AluOpType, ActivationFunctionType
 BF, F32, I32, U16 = "bfloat16", "float32", "int32", "uint16"
 NCH = 4
 BIG = 1024.0
-STYLE = [[0, 1, 1, 0], [1, 1, 1, 0], [1, 1, 1, 0], [1, 1, 0, 0]]
-VG = [[0, 1], [0, 1], [0], []]
-AHEAD = [[1, 2], [3], [], []]
+MODE = ["PAAP", "AAAP", "AAAP", "AAAA"]
+VG = [[[(1, 0), (1, 1)], [(1, 0), (1, 1)], [(1, 0), (2, 0)], [(2, 1)]],
+      [[(1, 0), (0, 0), (0, 1)], [(1, 0), (2, 0)], [(2, 1), (0, 0), (0, 1)], [(1, 0)]],
+      [[(0, 0), (0, 1)], [(1, 0), (3, 0), (2, 0)], [(2, 1), (0, 1)], [(1, 0)]],
+      [[(1, 0), (1, 1), (0, 0)], [(1, 0), (2, 0)], [(1, 0), (2, 1)], [(1, 0), (0, 1)]]]
+NAR = [[[(1, 0), (0, 0)], [], [(3, 1)], [(2, 1), (3, 1)]],
+       [[(3, 1)], [(1, 0)], [(1, 1)], [(2, 1), (0, 0), (0, 1), (3, 1)]],
+       [[(3, 1)], [(3, 0)], [], [(2, 1), (3, 1), (0, 1), (3, 0)]],
+       [[], [], [], []]]
+FIRSTH = [1, 1, 0, 0]
+LASTHALF = [[3, 0], [3, 2], [3], []]
 SPLIT = 1024
+CYC, WAKE, EPS, GCYC, BIAS, ADDUS, DW = 1.04e-3, 0.06, 0.1, 1.6, 3.0, 2.2, 0.5
+NND, NNF, NDMA = 4, 4, 12
 SCRATCH = {
     "pw": ("sbuf", [128, 4096], BF), "sw": ("sbuf", [128, 4096], I32), "sq": ("sbuf", [128, 1792], F32),
     "cq": ("sbuf", [128, 1792], BF),
@@ -23,14 +33,12 @@ SCRATCH = {
     "rt0": ("sbuf", [128, 24], BF), "rt1": ("sbuf", [128, 24], BF), "rt2": ("sbuf", [128, 24], BF),
     "rmin": ("sbuf", [128, 512], BF), "rmax": ("sbuf", [128, 512], BF),
     "ci": ("sbuf", [128, 16], I32), "cf": ("sbuf", [128, 16], F32),
-    "posc": ("sbuf", [128, 32], F32), "headc": ("sbuf", [128, 32], F32), "sbase": ("sbuf", [128, 32], F32), "sbf": ("sbuf", [128, 32], F32),
-    "t1": ("sbuf", [128, 8], F32), "t3": ("sbuf", [128, 8], F32), "offc": ("sbuf", [128, 32], U16), "offs": ("sbuf", [128, 32], U16),
-    "crow": ("sbuf", [128, 4, 128], BF), "own": ("sbuf", [128, 512], F32), "ns": ("sbuf", [128, 4, 8, 16], F32), "cr": ("sbuf", [128, 4, 8, 16], F32),
+    "posc": ("sbuf", [128, 4, 8], F32), "headc": ("sbuf", [128, 4, 8], F32), "sbase": ("sbuf", [128, 4, 8], F32), "sbf": ("sbuf", [128, 4, 8], F32),
+    "t1": ("sbuf", [128, 4, 8], F32), "t3": ("sbuf", [128, 4, 8], F32), "offc": ("sbuf", [128, 32], U16), "offs": ("sbuf", [128, 32], U16),
+    "crow": ("sbuf", [128, 4, 128], BF), "own": ("sbuf", [128, 512], F32), "ns": ("sbuf", [128, 4, 8, 16], F32), "cr": ("sbuf", [128, 8, 16], F32),
+    "nsx": ("sbuf", [128, 4, 16, 8], F32), "crx": ("sbuf", [128, 4, 16, 8], F32),
     "cn": ("sbuf", [128, 256], F32), "idx": ("sbuf", [128, 16, 4, 16], I32), "off": ("sbuf", [128, 1024], U16),
-    "flg": ("sbuf", [128, 128], BF), "dm": ("sbuf", [128, 128], BF),
     "ygb": ("sbuf", [128, 64, 8], F32), "ycb": ("sbuf", [128, 64, 8], F32),
-    "n0": ("sbuf", [128, 512], BF), "n1": ("sbuf", [128, 512], BF), "n2": ("sbuf", [128, 512], BF),
-    "fa": ("sbuf", [128, 512], BF), "fb": ("sbuf", [128, 512], BF),
     "d0": ("psum", [128, 512], F32), "d1": ("psum", [128, 512], F32), "d2": ("psum", [128, 512], F32), "d3": ("psum", [128, 512], F32),
     "ca0": ("psum", [128, 2, 4, 64], F32), "ca1": ("psum", [128, 2, 4, 64], F32),
     "jb": ("psum", [128, 4, 8, 16], F32), "mb": ("psum", [128, 4, 128], F32),
@@ -38,7 +46,10 @@ SCRATCH = {
 for _c in range(NCH):
     SCRATCH["e%d" % _c] = ("sbuf", [128, 4096], BF)
     SCRATCH["sc%d" % _c] = ("sbuf", [128, 8, 512], BF)
-NDMA = 12
+    SCRATCH["flg%d" % _c] = ("sbuf", [128, 128], BF)
+    SCRATCH["dm%d" % _c] = ("sbuf", [128, 128], BF)
+    SCRATCH["n%d" % _c] = ("sbuf", [128, 512], BF)
+    SCRATCH["f%d" % _c] = ("sbuf", [128, 512], BF)
 SEMAPHORES = ["sV", "sS", "sP", "sG", "loc"] + ["arr%d" % i for i in range(4)] + ["dma%d" % i for i in range(NDMA)] + ["add%d" % i for i in range(8)]
 
 
@@ -49,6 +60,79 @@ def slot(t, al, b):
     return (s * al + 4 * b) % 8
 
 
+def order(prog):
+    n = len(prog)
+    wr, rd, users = {}, {}, {}
+    succs, left = [[] for _ in range(n)], []
+    for i, p in enumerate(prog):
+        s = set(wr[k] for k in p["r"] + p["w"] if k in wr)
+        for k in p["w"]:
+            s.update(rd.get(k, ()))
+        s.discard(i)
+        for k in p["r"]:
+            rd.setdefault(k, []).append(i)
+        for k in p["w"]:
+            wr[k] = i
+            rd[k] = []
+        left.append(len(s))
+        for q in s:
+            succs[q].append(i)
+        for v in p["use"]:
+            users[v] = users.get(v, 0) + 1
+    path = [0.0] * n
+    for i in range(n - 1, -1, -1):
+        p = prog[i]
+        path[i] = p["us"] + p["lat"] + (p["dma"] * DW + 1.8 if p["dma"] else 0.0) + max([path[q] + WAKE for q in succs[i]] or [0.0])
+    rank = [path[i] - BIAS * prog[i]["c"] for i in range(n)]
+    at = [0.0] * n
+    ready = [i for i in range(n) if not left[i]]
+    qfree, bank, engines = {}, {}, 0.0
+    free = {k: 0.0 for k in range(4)}
+    where, seq = {}, []
+    while ready:
+        cand = []
+        for i in ready:
+            p = prog[i]
+            t = max(at[i], qfree.get(p["e"], 0.0))
+            if p["alloc"] is not None:
+                if not free:
+                    continue
+                t = max(t, min(free.values()) + WAKE)
+            for b in p["x"]:
+                if b in bank and bank[b][0] != p["e"]:
+                    t = max(t, bank[b][1] + WAKE)
+            cand.append((t, i))
+        best, i = min(cand)
+        e = prog[i]["e"]
+        t, i = max([c for c in cand if prog[c[1]]["e"] == e and c[0] <= best + EPS], key=lambda c: (rank[c[1]], -c[1]))
+        p = prog[i]
+        if p["alloc"] is not None:
+            k = min(free, key=lambda b: free[b])
+            where[p["alloc"]] = k
+            del free[k]
+        qfree[e] = t + p["us"]
+        if p["dma"]:
+            engines = max(t + 1.2, engines) + p["dma"]
+            end = engines + .6
+        else:
+            end = t + p["us"] + p["lat"]
+        for b in p["x"]:
+            bank[b] = (e, end)
+        for v in p["use"]:
+            users[v] -= 1
+            if not users[v]:
+                free[where[v]] = end
+        ready.remove(i)
+        seq.append(i)
+        for q in succs[i]:
+            left[q] -= 1
+            at[q] = max(at[q], end + WAKE)
+            if not left[q]:
+                ready.append(q)
+    assert len(seq) == n
+    return seq, where
+
+
 def rank_program(g, core, T, topo):
     rank = T.rank_of(core)
     if rank is None:
@@ -57,6 +141,48 @@ def rank_program(g, core, T, topo):
     COPY = ActivationFunctionType.Copy
     V, S, P = g.vector, g.scalar, g.tensor
     queue = {"V": V, "S": S, "P": P, "G": g, "Y": g.sync}
+
+    prog = []
+    now = [0]
+    where = {}
+
+    def rec(e, emit, r, w, x, us, lat=0.0, load=0.0, use=(), alloc=None):
+        prog.append({"e": e, "emit": emit, "r": list(r), "w": list(w), "x": list(x), "us": us, "lat": lat, "dma": load, "use": list(use), "alloc": alloc, "c": now[0]})
+
+    def op(e, calls, r=(), w=(), x=(), n=64, us=None, use=(), alloc=None, pre=None):
+        calls = calls if isinstance(calls, list) else [calls]
+
+        def emit():
+            if pre:
+                pre()
+            xs = list(x) + ["d%d" % where[v] for v in list(use) + ([alloc] if alloc is not None else [])]
+            need(e, deps(e, r, w, xs))
+            sem = "s" + e
+            for call in calls:
+                call().then_inc(T.sem[sem], 1)
+                count[sem] += 1
+            done(e, sem, count[sem], r, w, xs)
+        rec(e, emit, r, w, x, max(64, n) * CYC if us is None else us, 0.0, 0.0, use, alloc)
+
+    def dma(e, out, in_, r=(), w=(), load=0.5):
+        def emit():
+            need(e, deps("dma", r, w, ()))
+            sem = "dma%d" % ndma[0]
+            ndma[0] += 1
+            queue[e].dma_start(out, in_).then_inc(T.sem[sem], 16)
+            done(e, sem, 16, r, w)
+        rec(e, emit, r, w, (), .1, 0.0, load)
+
+    nadd = [0] * 8
+
+    def dma_add(i, out, in_, r, w):
+        def emit():
+            need("G", deps("dma", r, w, ()))
+            nadd[i] += 16
+            g.dma_start(out, in_, accum_op=A.add).then_inc(T.sem["add%d" % i], 16)
+            done("G", "add%d" % i, nadd[i], r, w)
+        rec("G", emit, r, w, (), 1.0, 0.0, ADDUS)
+
     count = {"sV": 0, "sS": 0, "sP": 0, "sG": 0}
     know = {e: {} for e in queue}
     snaps = {}
@@ -79,61 +205,25 @@ def rank_program(g, core, T, topo):
 
     def deps(e, r, w, x):
         own = "s" + e
-        tok = []
-        for k in r:
-            if k in wr:
-                tok.append(wr[k])
+        tok = [wr[k] for k in list(r) + list(w) if k in wr]
         for k in w:
-            if k in wr:
-                tok.append(wr[k])
-            for q in rd.get(k, ()):
-                if q[0] != own:
-                    tok.append(q)
+            tok += [q for q in rd.get(k, ()) if q[0] != own]
         for k in x:
-            for q in bank.get(k, {}).values():
-                if q[0] != own:
-                    tok.append(q)
+            tok += [q for q in bank.get(k, {}).values() if q[0] != own]
         return tok
-
-    def mark(tok, r, w, x):
-        for k in r:
-            lst = [q for q in rd.get(k, []) if q[0] != tok[0]]
-            lst.append(tok)
-            rd[k] = lst
-        for k in w:
-            wr[k] = tok
-            rd[k] = []
-        for k in x:
-            bank.setdefault(k, {})[tok[0]] = tok
 
     def done(e, sem, val, r, w, x=()):
         sn = dict(know[e])
         sn[sem] = val
         snaps[(sem, val)] = sn
-        mark((sem, val), r, w, x)
-
-    def op(e, calls, r=(), w=(), x=()):
-        need(e, deps(e, r, w, x))
-        sem = "s" + e
-        for call in (calls if isinstance(calls, list) else [calls]):
-            call().then_inc(T.sem[sem], 1)
-            count[sem] += 1
-        done(e, sem, count[sem], r, w, x)
-
-    def dma(e, out, in_, r=(), w=()):
-        need(e, deps("dma", r, w, ()))
-        sem = "dma%d" % ndma[0]
-        ndma[0] += 1
-        queue[e].dma_start(out, in_).then_inc(T.sem[sem], 16)
-        done(e, sem, 16, r, w)
-
-    nadd = [0] * 8
-
-    def dma_add(i, out, in_, r, w):
-        need("G", deps("dma", r, w, ()))
-        nadd[i] += 16
-        g.dma_start(out, in_, accum_op=A.add).then_inc(T.sem["add%d" % i], 16)
-        done("G", "add%d" % i, nadd[i], r, w)
+        tok = (sem, val)
+        for k in r:
+            rd[k] = [q for q in rd.get(k, []) if q[0] != sem] + [tok]
+        for k in w:
+            wr[k] = tok
+            rd[k] = []
+        for k in x:
+            bank.setdefault(k, {})[sem] = tok
 
     W = [T.w0, T.w1, T.w2, T.w3]
     D = [T.d0, T.d1, T.d2, T.d3]
@@ -160,8 +250,11 @@ def rank_program(g, core, T, topo):
     def mm(out, l, rhs, st, sp):
         return lambda: P.matmul(out, l, rhs, st, sp)
 
+    def gat(n):
+        return .05 + GCYC * CYC * n
+
     dma("Y", T.candl[:], T.cand[:], w=["candl"])
-    dma("Y", T.pw[:, 0:SPLIT], T.pe[:, 0:SPLIT], w=["pwa"])
+    dma("Y", T.pw[:, 0:SPLIT], T.pe[:, 0:SPLIT], w=["pwa", "yq"], load=1.0)
     dma("S", T.geoi[:], T.geo[:], w=["geoi"])
     dma("S", T.nbi[:], T.nb[:], w=["nbi"])
 
@@ -173,265 +266,313 @@ def rank_program(g, core, T, topo):
     def fcol(k):
         return cf[:, k:k + 1]
 
-    op("G", lambda: g.iota(icol(0), [[0, 1]], 0, 1), w=["ci0"])
-    op("G", lambda: g.iota(T.posc[:], [[1, 8], [448, 4]], 0, 0, allow_small_or_imprecise_dtypes=True), w=["posc"])
+    FREE = {"allow_small_or_imprecise_dtypes": True}
+    op("G", lambda: g.iota(icol(0), [[0, 1]], 0, 1), w=["ci0"], us=.13)
+    op("G", lambda: g.iota(T.posc[:], [[448, 4], [1, 8]], 0, 0, **FREE), w=["posc0", "posc3"], us=.2)
     op("V", ms(T.ones[:], 1.0), w=["ones"])
-    op("V", ms(T.cq[:], 0.0), w=["cq"])
-    op("G", lambda: g.affine_select(T.bt[:], T.ones[:], [[-16, 8], [0, 16]], A.is_ge, 0.0, 0, 1), r=["ones"], w=["bt"])
-    op("G", lambda: g.affine_select(T.bm[:], T.bt[:], [[16, 8], [0, 16]], A.is_ge, 0.0, 15, -1), r=["bt"], w=["bm"])
-    op("G", lambda: g.iota(T.qrow[:], [[0, 8], [1, 16]], 0, 0, allow_small_or_imprecise_dtypes=True), w=["qrow"])
-    op("G", lambda: g.affine_select(T.ip[:], T.ones[:], [[-1, 128]], A.is_equal, 0.0, 0, 1), r=["ones"], w=["ip"])
-    op("G", lambda: g.iota(T.headc[:], [[0, 8], [448, 4]], 8, 0, allow_small_or_imprecise_dtypes=True), w=["headc"])
-    op("G", lambda: g.iota(T.sbase[:], [[0, 8], [-7164, 4]], 0, 0, allow_small_or_imprecise_dtypes=True), w=["sbase"])
+    op("V", ms(T.cq[:], 0.0), w=["cq"], n=896)
+    op("G", lambda: g.affine_select(T.bt[:], T.ones[:], [[-16, 8], [0, 16]], A.is_ge, 0.0, 0, 1), r=["ones"], w=["bt"], us=.43)
+    op("G", lambda: g.affine_select(T.bm[:], T.bt[:], [[16, 8], [0, 16]], A.is_ge, 0.0, 15, -1), r=["bt"], w=["bm"], us=.43)
+    op("G", lambda: g.iota(T.qrow[:], [[0, 8], [1, 16]], 0, 0, **FREE), w=["qrow"], us=.4)
+    op("G", lambda: g.affine_select(T.ip[:], T.ones[:], [[-1, 128]], A.is_equal, 0.0, 0, 1), r=["ones"], w=["ip"], us=.43)
+    op("G", lambda: g.iota(T.headc[:], [[448, 4], [0, 8]], 8, 0, **FREE), w=["headc0", "headc3"], us=.2)
+    op("G", lambda: g.iota(T.sbase[:], [[-7164, 4], [0, 8]], 0, 0, **FREE), w=["sbase"], us=.2)
     op("V", ts(icol(1), icol(0), 15, A.bitwise_and), r=["ci0"], w=["ci1"])
     op("V", cp(fcol(1), icol(1)), r=["ci1"], w=["cf1"])
     op("V", ts(fcol(2), fcol(1), 28.0, A.mult), r=["cf1"], w=["cf2"])
     op("V", ts(fcol(3), fcol(1), 1.5, A.is_lt), r=["cf1"], w=["cf3"])
-    op("V", ts(T.posc[:], T.posc[:], fcol(2), A.add), r=["posc", "cf2"], w=["posc"])
-    op("V", ts(T.clo[:], T.candl[:], 63, A.bitwise_and), r=["candl"], w=["clo"])
-    op("V", tt(T.chib[:], T.candl[:], T.clo[:], A.subtract), r=["clo", "candl"], w=["chib"])
-    op("V", cp(T.clob[:], T.clo[:]), r=["clo"], w=["clob"])
-    dma("Y", T.cq[0:128:16, :], T.chib[:], r=["chib", "cq"], w=["cqh"])
-    dma("Y", T.cq[1:128:16, :], T.clob[:], r=["clob", "cq"], w=["cql"])
-    dma("Y", T.pw[:, SPLIT:4096], T.pe[:, SPLIT:4096], w=["pw"])
-    dma("Y", T.sw[:], T.se[:], w=["sw"])
-    op("V", ms(T.csel[:], 0.0), w=["csel"])
-    op("V", ms(T.casel[:], 0.0), w=["casel"])
+    op("V", ts(T.posc[:], T.posc[:], fcol(2), A.add), r=["posc0", "posc3", "cf2"], w=["posc0", "posc3"])
+    op("V", ts(T.clo[:], T.candl[:], 63, A.bitwise_and), r=["candl"], w=["clo"], n=112)
+    op("V", tt(T.chib[:], T.candl[:], T.clo[:], A.subtract), r=["clo", "candl"], w=["chib"], n=224)
+    op("V", cp(T.clob[:], T.clo[:]), r=["clo"], w=["clob"], n=112)
+    dma("Y", T.cq[0:128:16, :], T.chib[:], r=["chib", "cq", "yq"], w=["cqh", "cqw"])
+    dma("Y", T.cq[1:128:16, :], T.clob[:], r=["clob", "cq", "yq"], w=["cql", "cqv"])
+    dma("Y", T.pw[:, SPLIT:4096], T.pe[:, SPLIT:4096], w=["pw", "cqw"], load=2.4)
+    dma("Y", T.sw[:], T.se[:], w=["sw", "cqw"], load=6.5)
+    op("V", ms(T.csel[:], 0.0), w=["csel"], n=512)
+    op("V", ms(T.casel[:], 0.0), w=["casel"], n=128)
     op("V", ts(T.selk[:], T.bm[:], fcol(3), A.mult), r=["bm", "cf3"], w=["selk"])
     op("V", ts(T.m16[:], T.qrow[:, 0:16], fcol(1), A.is_equal), r=["qrow", "cf1"], w=["m16"])
     op("V", cp(T.geof[:], T.geoi[:]), r=["geoi"], w=["geof"])
-    op("V", cp(T.bf32[:], T.bm[:]), r=["bm"], w=["bf32"])
+    op("V", cp(T.bf32[:], T.bm[:]), r=["bm"], w=["bf32"], n=128)
     for u in range(8):
         op("V", cp(T.csel[:, u, :, u, :], T.selk[:, u:64:8, :]), r=["selk", "csel"], w=["cselu%d" % u])
     for b in range(2):
         op("V", cp(T.casel[:, b, :, b], T.selk[:, :, b]), r=["selk", "casel"], w=["caselb%d" % b])
-    GM = []
+    GM = ["gm%d%d" % (c, j) for c in range(NCH) for j in range(4)]
     for c in range(NCH):
         for j in range(4):
-            GM.append("gm%d%d" % (c, j))
-            op("V", ts(T.gm[:, 64 * c + 16 * j:64 * c + 16 * j + 16], T.m16[:], T.geof[:, 4 * j + c:4 * j + c + 1], A.mult), r=["m16", "geof"], w=[GM[-1]])
-    op("P", mm(T.jb[:, 2:4, :, :], T.bf32[:], T.gm[:], True, True), r=["bf32"] + GM, w=["jb"], x=["jb"])
+            lo = 64 * c + 16 * j
+            op("V", ts(T.gm[:, lo:lo + 16], T.m16[:], T.geof[:, 4 * j + c:4 * j + c + 1], A.mult), r=["m16", "geof"], w=["gm%d%d" % (c, j)])
+    op("P", mm(T.jb[:, 2:4, :, :], T.bf32[:], T.gm[:], True, True), r=["bf32"] + GM, w=["jbg"], x=["jb"], us=.8)
     for c in range(NCH):
         for al in range(4):
             o, i = T.geor[:, 4 * c + al, :, :], T.jb[:, 2 + c // 2, 4 * (c % 2):4 * (c % 2) + 4, :]
-            op("S", lambda o=o, i=i: S.activation(o, i, COPY, bias=-65536.0, scale=16.0), r=["jb"], w=["geor%d" % (4 * c + al)], x=["jb"])
-
-    def gather_codes(c):
-        op("V", cp(T.crow[:, c, :], T.cq[:].indirect(T.offc[:, 8 * c:8 * c + 8])),
-           r=["cq", "cqh", "cql", "offc%d" % c], w=["crow%d" % c])
-
-    ALLC = ["crow%d" % c for c in range(NCH)]
+            op("S", lambda o=o, i=i: S.activation(o, i, COPY, bias=-65536.0, scale=16.0), r=["jbg"], w=["geor%d" % (4 * c + al)], x=["jb"])
 
     def crow_of(a, t, c0=0, c1=NCH):
         return T.crow[:, c0:c1, 16 * a:16 * a + 16] if t else T.cq[:, a:1792:28]
 
     def crow_keys(t, c0=0, c1=NCH):
-        return ALLC[c0:c1] if t else ["cq", "cqh", "cql"]
+        return ["crow%d" % c for c in range(c0, c1)] if t else ["cq", "cqh", "cql"]
 
-    def code_sums(t, c0, c1):
-        op("P", [mm(T.mb[:, 1, 64 + 16 * c0:64 + 16 * c1], T.csel[:, u, :, :, :], crow_of(u, t, c0, c1), u == 0, u == 7) for u in range(8)],
-           r=crow_keys(t, c0, c1) + ["cselu%d" % u for u in range(8)], w=["mb"], x=["mb"])
+    nsig = [0] * 4
 
     def send_codes(t, c0, c1):
+        op("P", [mm(T.jb[:, 1, c0:c1, :], T.csel[:, u, :, :, :], crow_of(u, t, c0, c1), u == 0, u == 7) for u in range(8)],
+           r=crow_keys(t, c0, c1) + ["cselu%d" % u for u in range(8)], w=["jbc"], x=["jb"], us=.35)
         mine = W[t][:, 64 * rank + 16 * c0:64 * rank + 16 * c1]
         key = "wown%d%d" % (t, c0)
-        op("V", cp(mine, T.mb[:, 1, 64 + 16 * c0:64 + 16 * c1]), r=["mb"], w=[key], x=["mb"])
-        need("G", deps("G", [key], [], []))
-        m = topo.mask(core, others[0])
-        ids = []
-        for o in others:
-            m &= topo.mask(core, o)
-            a = topo.addr(o)
-            ids.append(DstId(rid=a[0], pnc=a[1]))
-        tr = RemoteDMATransfer(dst_ids=ids, dma_engine_mask=m, remote_sem=T.sem["arr%d" % t], srcs=[mine], dsts=[mine for _ in ids])
-        g.remote_dma_fused([tr], local_sem=T.sem.loc)
-        return bin(m).count("1")
+        op("V", cp(mine, T.jb[:, 1, c0:c1, :]), r=["jbc"], w=[key], x=["jb"])
+
+        def emit():
+            need("G", deps("G", [key], [], []))
+            m = topo.mask(core, others[0])
+            ids = []
+            for o in others:
+                m &= topo.mask(core, o)
+                a = topo.addr(o)
+                ids.append(DstId(rid=a[0], pnc=a[1]))
+            tr = RemoteDMATransfer(dst_ids=ids, dma_engine_mask=m, remote_sem=T.sem["arr%d" % t], srcs=[mine], dsts=[mine for _ in ids])
+            g.remote_dma_fused([tr], local_sem=T.sem.loc)
+            nsig[t] += bin(m).count("1")
+        rec("G", emit, [key], ["sent%d%d" % (t, c0)], [], .6, 3.0 if t else 5.0)
 
     def own_codes(t):
         for al in range(4):
-            calls = []
-            for j in range(4):
-                for b in range(2):
-                    calls.append(mm(CA[al // 2][:, al % 2, j, :], T.casel[:, b, :, :], crow_of(slot(t, al, b), t), b == 0, b == 1))
-            op("P", calls, r=crow_keys(t) + ["caselb0", "caselb1"], w=["ca%d" % al], x=["cab%d" % (al // 2)])
-
-    def self_list():
-        op("V", ts(T.sbf[:], T.posc[:], 16.0, A.mult), r=["posc"], w=["sbf"])
-        op("V", tt(T.sbf[:], T.sbf[:], T.sbase[:], A.add), r=["sbf", "sbase"], w=["sbf"])
-        op("V", cp(T.offs[:], T.sbf[:]), r=["sbf"], w=["offs"])
-
-    def self_gather():
-        op("S", lambda: S.activation(T.own[:], T.sq[:].indirect(T.offs[:]), COPY), r=["sq", "offs"], w=["own"])
+            calls = [mm(CA[al // 2][:, al % 2, j, :], T.casel[:, b, :, :], crow_of(slot(t, al, b), t), b == 0, b == 1) for j in range(4) for b in range(2)]
+            op("P", calls, r=crow_keys(t) + ["caselb0", "caselb1"], w=["ca%d" % al] + ["pr%d" % (4 * c + al) for c in range(NCH)], x=["cab%d" % (al // 2)], us=.35)
 
     def self_gaps(t):
+        op("V", ts(T.sbf[:], T.posc[:], 16.0, A.mult), r=["posc0", "posc3"], w=["sbf"])
+        op("V", tt(T.sbf[:], T.sbf[:], T.sbase[:], A.add), r=["sbf", "sbase"], w=["sbf"])
+        for c in range(NCH):
+            op("V", cp(T.offs[:, c:32:4], T.sbf[:, c, :]), r=["sbf"], w=["offs%d" % c])
+        op("S", lambda: S.activation(T.own[:], T.sq[:].indirect(T.offs[:]), COPY), r=["sq"] + ["offs%d" % c for c in range(NCH)], w=["own"], us=gat(512))
         for k in range(8):
             a = slot(t, k // 2, k % 2)
             b = (a + 1 + t) % 8
-            op("V", tt(T.ns[:, :, k, :], T.own[:, 64 * b:64 * b + 64], T.own[:, 64 * a:64 * a + 64], A.subtract), r=["own"], w=["ns%d" % k])
+            if t < 3:
+                op("V", tt(T.ns[:, :, k, :], T.own[:, 64 * b:64 * b + 64], T.own[:, 64 * a:64 * a + 64], A.subtract), r=["own"], w=["ns%d" % k], n=128)
+            else:
+                op("V", tt(T.nsx[:, 0:3, :, k], T.own[:, 64 * b:64 * b + 48], T.own[:, 64 * a:64 * a + 48], A.subtract), r=["own"], w=["nsx%d" % k], n=96)
+                op("V", tt(T.ns[:, 3, k, :], T.own[:, 64 * b + 48:64 * b + 64], T.own[:, 64 * a + 48:64 * a + 64], A.subtract), r=["own"], w=["ns%d" % k])
 
     NS = ["ns%d" % k for k in range(8)]
+    NX = ["nsx%d" % k for k in range(8)]
+    MB = ["mbp%d" % c for c in range(NCH)]
 
-    def code_rows(t):
-        op("P", [mm(T.mb[:], T.selk[:], T.crow[:], True, True)], r=ALLC + ["selk"], w=["mb"], x=["mb"])
-        for k in range(8):
-            a = slot(t, k // 2, k % 2)
-            op("V", cp(T.cr[:, :, k, :], T.mb[:, :, 16 * a:16 * a + 16]), r=["mb"], w=["cr%d" % k], x=["mb"])
+    def code_rows():
+        op("P", [mm(T.mb[:], T.selk[:], T.crow[:], True, True)], r=crow_keys(3) + ["selk"], w=MB, x=["mb"], us=.3)
+        for a in range(8):
+            op("V", cp(T.crx[:, 0:3, :, a], T.mb[:, 0:3, 16 * a:16 * a + 16]), r=MB, w=["crx%d" % a], x=["mb"])
+            op("V", cp(T.cr[:, a, :], T.mb[:, 3, 16 * a:16 * a + 16]), r=MB, w=["cr%d" % a], x=["mb"])
+
+    waited = {}
 
     def neighbours(t, c0, c1):
-        op("V", cp(T.cn[:, 64 * c0:64 * c1], W[t][:].indirect(T.nbu[:, 4 * c0:4 * c1])), r=["nbu", "wown%d0" % t, "wown%d3" % t],
-           w=["cn%d" % c for c in range(c0, c1)])
+        def pre():
+            if t not in waited:
+                waited[t] = 1
+                V.wait_ge(T.sem["arr%d" % t], 3 * nsig[t])
+        op("V", cp(T.cn[:, 64 * c0:64 * c1], W[t][:].indirect(T.nbu[:, 4 * c0:4 * c1])), r=["nbu", "wown%d0" % t, "wown%d3" % t, "sent%d0" % t, "sent%d3" % t],
+           w=["cn%d" % c for c in range(c0, c1)], us=gat(64 * (c1 - c0)), pre=pre)
 
-    def index(c, first=()):
-        def product(al):
-            ca = CA[al // 2][:, al % 2, :, 16 * c:16 * c + 16]
-            op("V", tt(ca, T.cn[:, 64 * c:64 * c + 64], ca, A.mult), r=["cn%d" % c, "ca%d" % al], w=["pr%d" % (4 * c + al)], x=["cab%d" % (al // 2)])
-
-        def shift(al):
-            k = 4 * c + al
-            ca = CA[al // 2][:, al % 2, :, 16 * c:16 * c + 16]
-            op("V", tt(T.idx[:, k, :, :], ca, T.geor[:, k, :, :], A.add), r=["pr%d" % k, "geor%d" % k], w=["ix%d" % k], x=["cab%d" % (al // 2)])
-
-        def wrap(ks):
+    def index(c, groups):
+        for als in groups:
+            ks = [4 * c + al for al in als]
+            for al in als:
+                ca = CA[al // 2][:, al % 2, :, 16 * c:16 * c + 16]
+                op("V", tt(ca, T.cn[:, 64 * c:64 * c + 64], ca, A.mult), r=["cn%d" % c, "ca%d" % al], w=["pr%d" % (4 * c + al)], x=["cab%d" % (al // 2)])
+            for al in als:
+                k = 4 * c + al
+                ca = CA[al // 2][:, al % 2, :, 16 * c:16 * c + 16]
+                op("V", tt(T.idx[:, k, :, :], ca, T.geor[:, k, :, :], A.add), r=["pr%d" % k, "geor%d" % k], w=["ix%d" % k], x=["cab%d" % (al // 2)])
+            IX = ["ix%d" % k for k in ks]
             v = T.idx[:, ks[0]:ks[-1] + 1, :, :]
-            op("V", ts(v, v, 4, A.arith_shift_right, 4095, A.bitwise_and), r=["ix%d" % k for k in ks], w=["ix%d" % k for k in ks])
-
-        def narrow(ks):
-            op("V", cp(T.off[:, 64 * ks[0]:64 * ks[-1] + 64], T.idx[:, ks[0]:ks[-1] + 1, :, :]), r=["ix%d" % k for k in ks], w=["of%d" % k for k in ks])
-
-        if not first:
-            ks = [4 * c + al for al in range(4)]
-            for al in range(4):
-                product(al)
-            for al in range(4):
-                shift(al)
-            wrap(ks)
-            narrow(ks)
-        else:
-            for als in ([first[0]], first[1:]):
-                for al in als:
-                    product(al)
-                for al in als:
-                    shift(al)
-                for al in als:
-                    wrap([4 * c + al])
-                for al in als:
-                    narrow([4 * c + al])
+            op("V", ts(v, v, 4, A.arith_shift_right, 4095, A.bitwise_and), r=IX, w=IX, n=64 * len(ks))
+            op("V", cp(T.off[:, 64 * ks[0]:64 * ks[-1] + 64], v), r=IX, w=["of%d" % k for k in ks], n=64 * len(ks))
 
     def gather(c, al, hs, sign=1.0, e="S"):
         k = 4 * c + al
         lo, n = 64 * k + 32 * hs[0], 32 * len(hs)
         out, src = E[c][:, 16 * lo - 4096 * c:16 * (lo + n) - 4096 * c], T.pw[:].indirect(T.off[:, lo:lo + n])
-        call = cp(out, src) if e == "V" else (lambda: S.activation(out, src, COPY, scale=sign))
-        op(e, call, r=["pw", "pwa", "of%d" % k], w=["e%d%d%d" % (c, al, h) for h in hs])
+        if e == "V":
+            call = cp(out, src) if sign == 1.0 else ts(out, src, sign, A.mult)
+        else:
+            call = lambda: S.activation(out, src, COPY, scale=sign)
+        op(e, call, r=["pw", "pwa", "of%d" % k], w=["e%d%d%d" % (c, al, h) for h in hs], us=gat(16 * n))
 
     def added(c, i, into, what):
         p, q = 1024 * into, 1024 * what
         dma_add(2 * c + i, E[c][:, p:p + 1024], E[c][:, q:q + 1024], ["e%d%d%d" % (c, what, h) for h in range(2)], ["e%d%d%d" % (c, into, h) for h in range(2)])
 
     def held(c, al, h):
-        return (E[c], "e%d%d%d" % (c, al, h), False, 1024 * al + 512 * h)
+        return (E[c], "e%d%d%d" % (c, al, h), 0, 1024 * al + 512 * h)
 
-    nd = [0]
+    nv, nn, nf = [0], [0], [0]
 
-    def pe_diff(c, h, plus, minus, flip=False, negated=False):
-        i = nd[0] % 4
-        nd[0] += 1
-        lp, lm = (T.im, T.ip) if negated else (T.ip, T.im)
-        calls = []
-        for j in range(2):
-            for b in range(2):
-                o = D[i][:, 256 * j + 128 * b:256 * j + 128 * b + 128]
-                p, q = [1024 * al + 512 * h + 256 * j for al in (plus, minus)]
-                b2 = 1 - b if flip else b
-                calls.append(mm(o, lp[:], E[c][:, p + b:p + 256:2], True, False))
-                calls.append(mm(o, lm[:], E[c][:, q + b2:q + 256:2], False, True))
-        op("P", calls, r=["e%d%d%d" % (c, plus, h), "e%d%d%d" % (c, minus, h), "ip", "im"], w=["d%d" % i], x=["d%d" % i])
-        return (D[i], "d%d" % i, True, 0)
+    def bank_diff(terms, r):
+        v = nv[0]
+        nv[0] += 1
 
-    def narrowed(i, src):
-        out = T["n%d" % i]
-        op("S", lambda: S.activation(out[:], src[0][:], COPY), r=[src[1]], w=["n%d" % i], x=[src[1]])
+        def call(j, b, i):
+            buf, col, fl, sg = terms[i]
+            lo = col + 256 * j
+            rhs = buf[:, lo + (1 - b if fl else b):lo + 256:2]
+            o = 256 * j + 128 * b
+            return lambda: P.matmul(D[where[v]][:, o:o + 128], (T.ip if sg > 0 else T.im)[:], rhs, i == 0, i == len(terms) - 1)
+        calls = [call(j, b, i) for j in range(2) for b in range(2) for i in range(len(terms))]
+        op("P", calls, r=list(r) + ["ip", "im"], w=["vd%d" % v], us=.085 * len(calls), alloc=v)
+        return (v, "vd%d" % v, 1, 0)
+
+    def narrowed(src):
+        i = nn[0] % NND
+        nn[0] += 1
+        out, v = T["n%d" % i], src[0]
+        op("S", lambda: S.activation(out[:], D[where[v]][:], COPY), r=[src[1]], w=["n%d" % i], use=[v], n=512)
         return (out, "n%d" % i, 2, 0)
 
-    def fused(c, h, other, out, key):
-        k = 4 * c + 1
+    def fused(c, h, al, other):
+        i = nf[0] % NNF
+        nf[0] += 1
+        out, key = T["f%d" % i], "f%d" % i
+        k = 4 * c + al
         lo = 64 * k + 32 * h
         p = 1024 * other + 512 * h
-        op("V", tt(out[:], T.pw[:].indirect(T.off[:, lo:lo + 32]), E[c][:, p:p + 512], A.subtract), r=["pw", "pwa", "of%d" % k, "e%d%d%d" % (c, other, h)], w=[key])
-        return (out, key, False, 0)
+        op("V", tt(out[:], T.pw[:].indirect(T.off[:, lo:lo + 32]), E[c][:, p:p + 512], A.subtract), r=["pw", "pwa", "of%d" % k, "e%d%d%d" % (c, other, h)], w=[key], us=gat(512))
+        return (out, key, 0, 0)
 
     def scan(c, al, h, src, low):
         rp = T.rmin if low else T.rmax
         o0, o1 = (A.max, A.min) if low else (A.min, A.max)
         k = 4 * h + al
-        if src[2]:
+        if src[2] == 1:
+            calls = [lambda: V.tensor_tensor_scan(SC[c][:, k, :], rp[:], D[where[src[0]]][:], 0.0, o0, o1)]
+        elif src[2] == 2:
             calls = [lambda: V.tensor_tensor_scan(SC[c][:, k, :], rp[:], src[0][:], 0.0, o0, o1)]
         else:
             calls = [lambda j=j, b=b: V.tensor_tensor_scan(SC[c][:, k, 256 * j + 128 * b:256 * j + 128 * b + 128], rp[:, 0:128],
                                                            src[0][:, src[3] + 256 * j + b:src[3] + 256 * j + 256:2], 0.0, o0, o1) for j in range(2) for b in range(2)]
-        op("V", calls, r=[src[1], "rmin" if low else "rmax"], w=["sc%d%d%d" % (c, al, h)], x=[src[1]] if src[2] is True else [])
+        op("V", calls, r=[src[1], "rmin" if low else "rmax"], w=["sc%d%d%d" % (c, al, h)], use=[src[0]] if src[2] == 1 else [], us=(512 if src[2] == 1 else 256) * CYC)
 
-    def sums(t, c):
-        for h in range(2):
-            if t < 3:
-                scan(c, 0, h, held(c, 1, h), False)
-                scan(c, 2, h, held(c, 2, h), True)
-            else:
-                for al in range(2):
-                    scan(c, al, h, held(c, al, h), True)
-                    scan(c, al + 2, h, held(c, al, h), False)
-
-    def jsum(t, c):
-        sets = [(0, 1, False), (1, 4, True)] if t < 3 else [(0, 2, True), (2, 4, False)]
+    def jsum(c, sets):
         calls = []
-        for a0, a1, pos in sets:
+        for k0, k1, low in sets:
             for j in range(4):
                 h, lo = 4 * (j // 2), 256 * (j % 2)
-                calls.append(mm(T.jb[:, 0, 2 * a0:2 * a1, :], (T.ip if pos else T.im)[:], SC[c][:, h + a0:h + a1, lo + 7:lo + 256:8], j == 0, j == 3))
-        op("P", calls, r=["ip", "im"] + ["sc%d%d%d" % (c, al, h) for al in range(4) for h in range(2)], w=["jb"], x=["jb"])
+                calls.append(mm(T.jb[:, 0, 2 * k0:2 * k1, :], (T.ip if low else T.im)[:], SC[c][:, h + k0:h + k1, lo + 7:lo + 256:8], j == 0, j == 3))
+        op("P", calls, r=["ip", "im"] + ["sc%d%d%d" % (c, al, h) for al in range(4) for h in range(2)], w=["jbs"], x=["jb"], us=.045 * len(calls))
 
-    def post(t, c):
-        def s0():
-            jsum(t, c)
+    def chunk(t, c):
+        flip = (t != 1)
+        onv, nar = VG[t][c], NAR[t][c]
+        vg = [h for h in range(2) if (1, h) in onv]
+        a = MODE[t][c] == "A"
+        first = [FIRSTH[t], 1 - FIRSTH[t]]
+        halves = [[h] for h in first] if c in LASTHALF[t] else [[0, 1]]
 
-        def s1():
-            op("V", tt(T.flg[:], T.jb[:, 0, :, :], T.ns[:, c, :, :], A.is_gt), r=["jb"] + NS, w=["flg"], x=["jb"])
-            if t == 3:
-                for k in range(8):
-                    op("V", tt(T.ygb[:, 16 * c:16 * c + 16, slot(t, k // 2, k % 2)], T.jb[:, 0, k, :], T.ns[:, c, k, :], A.subtract), r=["jb"] + NS, w=["yg%d%d" % (c, k)], x=["jb"])
+        def gathers(al, hs, sign=1.0, skip=()):
+            for e in "VS":
+                h2 = [h for h in hs if ((al, h) in onv) == (e == "V") and h not in skip]
+                if h2:
+                    gather(c, al, h2, sign, e)
 
-        def s2():
-            if t < 3:
-                op("P", mm(T.mb[:, 0, :], T.flg[:], T.bm[:], True, True), r=["flg", "bm"], w=["mb"], x=["mb"])
-            else:
-                op("P", [mm(T.mb[:, 0, :], T.kc[:], T.ones[:], True, False), mm(T.mb[:, 0, :], T.bn[:], T.flg[:], False, True)],
-                   r=["flg", "bn", "kc", "ones"], w=["mb"], x=["mb"])
+        def diff(k, h, p, q, sp, sq, fl=False):
+            d = bank_diff([(E[c], 1024 * p + 512 * h, False, sp), (E[c], 1024 * q + 512 * h, fl, sq)], ["e%d%d%d" % (c, p, h), "e%d%d%d" % (c, q, h)])
+            return narrowed(d) if (k, h) in nar else d
 
-        def s3():
-            if t < 3:
-                op("V", tt(T.dm[:], T.mb[:, 0, :], T.thr[:], A.is_ge), r=["mb", "thr"], w=["dm"], x=["mb"])
-            else:
-                for k in range(8):
-                    op("V", tt(T.ycb[:, 16 * c:16 * c + 16, slot(t, k // 2, k % 2)], T.mb[:, 0, 16 * k:16 * k + 16], T.cr[:, c, k, :], A.min), r=["mb", "cr%d" % k], w=["yc%d%d" % (c, k)], x=["mb"])
+        if t < 3 and a:
+            for al, sign in ((2, -1.0), (1, 1.0), (0, -1.0), (3, 1.0)):
+                for hs in halves:
+                    gathers(al, hs, sign)
+            m12 = [diff(1, h, 1, 2, 1, 1) for h in range(2)]
+            added(c, 0, 1, 0)
+            m30 = [diff(3, h, 3, 0, 1, 1, flip) for h in range(2)]
+            added(c, 1, 2, 3)
+            for al, src, low in ((1, m12, True), (3, m30, True), (0, [held(c, 1, h) for h in range(2)], False), (2, [held(c, 2, h) for h in range(2)], False)):
+                for h in range(2):
+                    scan(c, al, h, src[h], low)
+            return [(0, 1, False), (1, 2, True), (2, 3, False), (3, 4, True)]
+        if t < 3:
+            for hs in halves:
+                for al in range(4):
+                    gathers(al, hs, 1.0, vg if al == 1 else ())
+            for h in first:
+                if h in vg:
+                    f = fused(c, h, 1, 0)
+                    d = bank_diff([(f[0], 0, False, 1), (E[c], 512 * h, False, 1), (E[c], 2048 + 512 * h, False, -1)], [f[1], "e%d0%d" % (c, h), "e%d2%d" % (c, h)])
+                    d = narrowed(d) if (1, h) in nar else d
+                else:
+                    f = diff(0, h, 1, 0, 1, -1)
+                    d = None
+                scan(c, 0, h, f, False)
+                scan(c, 1, h, d or diff(1, h, 1, 2, 1, -1), True)
+                scan(c, 2, h, diff(2, h, 2, 3, 1, -1), True)
+                scan(c, 3, h, diff(3, h, 3, 0, 1, -1, flip), True)
+            return [(0, 1, False), (1, 4, True)]
+        gathers(3, [0, 1], 1.0 if vg else -1.0)
+        gathers(1, [0, 1], 1.0, vg)
+        if not vg:
+            added(c, 1, 1, 3)
+        gathers(2, [0, 1], -1.0)
+        gathers(0, [0, 1])
+        added(c, 0, 0, 2)
+        for h in range(2):
+            s = fused(c, h, 1, 3) if h in vg else (diff(1, h, 1, 3, 1, -1) if vg else held(c, 1, h))
+            scan(c, 1, h, s, True)
+            scan(c, 3, h, s, False)
+        for h in range(2):
+            scan(c, 0, h, held(c, 0, h), True)
+            scan(c, 2, h, held(c, 0, h), False)
+        return [(0, 2, True), (2, 4, False)]
 
-        def s4():
-            if t < 3:
-                op("P", mm(T.mb[:, 1, 0:24], T.dm[:], RT[t][:], True, True), r=["dm", "rt%d" % t], w=["mb"], x=["mb"])
+    def outputs(c, sets):
+        calls = []
+        for k0, k1, low in sets:
+            for k in range(2 * k0, 2 * k1):
+                for j in range(4):
+                    lo = 256 * (j % 2) + 128 * (k % 2)
+                    calls.append(mm(T.mb[:, 0, k:128:8], (T.ip if low else T.im)[:], SC[c][:, 4 * (j // 2) + k // 2, lo + 7:lo + 128:8], j == 0, j == 3))
+        op("P", calls, r=["ip", "im"] + ["sc%d%d%d" % (c, al, h) for al in range(4) for h in range(2)], w=["mbp0"], x=["mb"], us=.045 * len(calls))
+        flg = T["flg%d" % c]
+        op("V", tt(flg[:], T.mb[:, 0, :], T.nsx[:, c, :, :], A.is_gt), r=["mbp0"] + NX, w=["flg%d" % c], x=["mb"], n=128)
+        op("P", [mm(T.mb[:, 1, :], T.kc[:], T.ones[:], True, False), mm(T.mb[:, 1, :], T.bn[:], flg[:], False, True)],
+           r=["flg%d" % c, "bn", "kc", "ones"], w=["mbp1"], x=["mb"], us=.15)
+        op("V", tt(T.ygb[:, 16 * c:16 * c + 16, :], T.mb[:, 0, :], T.nsx[:, c, :, :], A.subtract), r=["mbp0"] + NX, w=["yg%d" % c], x=["mb"], n=128)
+        op("V", tt(T.ycb[:, 16 * c:16 * c + 16, :], T.mb[:, 1, :], T.crx[:, c, :, :], A.min), r=["mbp1"] + ["crx%d" % k for k in range(8)], w=["yc%d" % c], x=["mb"], n=128)
 
-        def s5():
-            if t < 3:
-                p, h = T.posc[:, c:32:4], T.headc[:, c:32:4]
-                op("V", tt(T.t1[:], T.mb[:, 1, 0:8], p, A.add), r=["mb", "posc"], w=["t1"], x=["mb"])
-                op("V", tt(T.t3[:], T.mb[:, 1, 8:16], h, A.add), r=["mb", "headc"], w=["t3"], x=["mb"])
-                op("V", tt(p, T.t1[:], T.t3[:], A.min), r=["t1", "t3"], w=["posc"])
-                op("V", cp(T.offc[:, 8 * c:8 * c + 8], p), r=["posc"], w=["offc%d" % c])
-                gather_codes(c)
-                op("V", tt(h, T.mb[:, 1, 16:24], h, A.add), r=["mb", "headc"], w=["headc"], x=["mb"])
-        return [s0, s1, s2, s3, s4, s5]
+    def post(t, c, sets):
+        if t == 3 and c < 3:
+            outputs(c, sets)
+            return
+        jsum(c, sets)
+        flg, dm = T["flg%d" % c], T["dm%d" % c]
+        op("V", tt(flg[:], T.jb[:, 0, :, :], T.ns[:, c, :, :], A.is_gt), r=["jbs"] + NS, w=["flg%d" % c], x=["jb"], n=128)
+        if t == 3:
+            for k in range(8):
+                op("V", tt(T.ygb[:, 16 * c:16 * c + 16, k], T.jb[:, 0, k, :], T.ns[:, c, k, :], A.subtract), r=["jbs"] + NS, w=["yg%d%d" % (c, k)], x=["jb"])
+            op("P", [mm(T.mb[:, 0, :], T.kc[:], T.ones[:], True, False), mm(T.mb[:, 0, :], T.bn[:], flg[:], False, True)],
+               r=["flg%d" % c, "bn", "kc", "ones"], w=["mbp0"], x=["mb"], us=.15)
+            for k in range(8):
+                op("V", tt(T.ycb[:, 16 * c:16 * c + 16, k], T.mb[:, 0, 16 * k:16 * k + 16], T.cr[:, k, :], A.min), r=["mbp0", "cr%d" % k], w=["yc%d%d" % (c, k)], x=["mb"])
+            return
+        op("P", mm(T.jb[:, 2, :, :], flg[:], T.bm[:], True, True), r=["flg%d" % c, "bm"], w=["jbg"], x=["jb"], us=.08)
+        op("V", tt(dm[:], T.jb[:, 2, :, :], T.thr[:], A.is_ge), r=["jbg", "thr"], w=["dm%d" % c], x=["jb"], n=128)
+        op("P", mm(T.mb[:, c, 0:24], dm[:], RT[t][:], True, True), r=["dm%d" % c, "rt%d" % t], w=["mbp%d" % c], x=["mb"], us=.06)
 
-    nsig = [0] * 4
-    code_sums(0, 0, NCH)
-    nsig[0] += send_codes(0, 0, NCH)
+    def places(c0, c1):
+        p, h, k = T.posc[:, c0:c1, :], T.headc[:, c0:c1, :], c0
+        P3 = MB[c0:c1]
+        op("V", tt(T.t1[:, c0:c1, :], T.mb[:, c0:c1, 0:8], p, A.add), r=P3 + ["posc%d" % k], w=["t1%d" % k], x=["mb"])
+        op("V", tt(T.t3[:, c0:c1, :], T.mb[:, c0:c1, 8:16], h, A.add), r=P3 + ["headc%d" % k], w=["t3%d" % k], x=["mb"])
+        op("V", tt(p, T.t1[:, c0:c1, :], T.t3[:, c0:c1, :], A.min), r=["t1%d" % k, "t3%d" % k], w=["posc%d" % k])
+        op("V", cp(T.offc[:, 8 * c0:8 * c1], p), r=["posc%d" % k], w=["offc%d" % k])
+        for c in range(c0, c1):
+            op("V", cp(T.crow[:, c, :], T.cq[:].indirect(T.offc[:, 8 * c:8 * c + 8])), r=["cq", "cqh", "cql", "offc%d" % k], w=["crow%d" % c], us=gat(128))
+        op("V", tt(h, T.mb[:, c0:c1, 16:24], h, A.add), r=P3 + ["headc%d" % k], w=["headc%d" % k], x=["mb"])
+
+    send_codes(0, 0, NCH)
     own_codes(0)
 
     for j in range(4):
@@ -443,15 +584,15 @@ def rank_program(g, core, T, topo):
     op("V", cp(fcol(0), icol(0)), r=["ci0"], w=["cf0"])
     for k in (3, 4, 5, 6):
         op("V", cp(fcol(k + 2), icol(k)), r=["ci%d" % k], w=["cf%d" % (k + 2)])
-    op("V", ms(T.rmin[:], -BIG), w=["rmin"])
-    op("V", ms(T.rmax[:], BIG), w=["rmax"])
+    op("V", ms(T.rmin[:], -BIG), w=["rmin"], n=256)
+    op("V", ms(T.rmax[:], BIG), w=["rmax"], n=256)
     op("V", ts(T.im[:], T.ip[:], -1.0, A.mult), r=["ip"], w=["im"])
     op("V", ts(fcol(9), fcol(6), 4.0, A.mult), r=["cf6"], w=["cf9"])
     op("V", ts(fcol(11), fcol(5), 2.0, A.mult), r=["cf5"], w=["cf11"])
     op("V", ts(fcol(12), fcol(5), 3.0, A.mult), r=["cf5"], w=["cf12"])
     op("V", ms(T.rmin[:, 0:512:8], BIG), w=["rmin"])
     op("V", ms(T.rmax[:, 0:512:8], -BIG), w=["rmax"])
-    op("V", ts(T.headc[:], T.headc[:], fcol(2), A.add), r=["headc", "cf2"], w=["headc"])
+    op("V", ts(T.headc[:], T.headc[:], fcol(2), A.add), r=["headc0", "headc3", "cf2"], w=["headc0", "headc3"])
     op("V", tt(fcol(10), fcol(9), fcol(5), A.add), r=["cf9", "cf5"], w=["cf10"])
     op("V", tt(fcol(11), fcol(11), fcol(6), A.add), r=["cf11", "cf6"], w=["cf11"])
     op("V", tt(icol(7), fcol(12), fcol(9), A.add), r=["cf12", "cf9"], w=["ci7"])
@@ -463,190 +604,53 @@ def rank_program(g, core, T, topo):
         op("V", ts(RT[t][:, 0:8], T.qrow[:, 0:8], a, A.is_equal, 4096.0, A.mult), r=["qrow", k], w=["rta%d" % t])
         op("V", ts(RT[t][:, 8:16], T.qrow[:, 0:8], a, A.is_gt), r=["qrow", k], w=["rtb%d" % t])
         op("V", ms(RT[t][:, 16:24], 1.0), r=["rta%d" % t, "rtb%d" % t], w=["rt%d" % t])
-    op("V", ts(T.thr[:], T.qrow[:], fcol(1), A.not_equal, 1000.0, A.mult), r=["qrow", "cf1"], w=["thr"])
+    op("V", ts(T.thr[:], T.qrow[:], fcol(1), A.not_equal, 1000.0, A.mult), r=["qrow", "cf1"], w=["thr"], n=128)
     op("V", ts(fcol(13), fcol(7), 448.0, A.mult), r=["cf7"], w=["cf13"])
     op("V", ts(fcol(14), fcol(1), -448.0, A.mult), r=["cf1"], w=["cf14"])
-    op("V", ts(T.thr[:], T.thr[:], 15.5, A.max), r=["thr"], w=["thr"])
+    op("V", ts(T.thr[:], T.thr[:], 15.5, A.max), r=["thr"], w=["thr"], n=128)
     op("V", tt(fcol(13), fcol(13), fcol(8), A.add), r=["cf13", "cf8"], w=["cf13"])
-    op("V", cp(T.cand16[:], T.candl[:]), r=["candl"], w=["cand16"])
+    op("V", cp(T.cand16[:], T.candl[:]), r=["candl"], w=["cand16"], n=112)
     op("V", tt(fcol(13), fcol(13), fcol(14), A.add), r=["cf13", "cf14"], w=["cf13"])
     op("V", ts(T.sbase[:], T.sbase[:], fcol(13), A.add), r=["sbase", "cf13"], w=["sbase"])
-
-    def last_constants():
-        op("V", ts(T.bn[:], T.bm[:], -4096.0, A.mult), r=["bm"], w=["bn"])
-        op("V", ts(fcol(14), fcol(0), 0.0, A.is_equal, 65536.0, A.mult), r=["cf0"], w=["cf14"])
-        op("V", ts(fcol(15), fcol(0), 1.0, A.is_equal), r=["cf0"], w=["cf15"])
-        op("V", tt(fcol(14), fcol(14), fcol(15), A.subtract), r=["cf14", "cf15"], w=["cf14"])
-        op("V", ts(T.kc[:], T.ones[:], fcol(14), A.mult), r=["ones", "cf14"], w=["kc"])
+    op("V", cp(T.sq[:], T.sw[:].indirect(T.cand16[:])), r=["sw", "cand16"], w=["sq"], us=gat(1792))
+    self_gaps(0)
 
     for t in range(4):
-        V.wait_ge(T.sem["arr%d" % t], 3 * nsig[t])
-        flip = (t != 1)
-        style = STYLE[t]
-        vg = [VG[c] if style[c] else [] for c in range(NCH)]
         neighbours(t, 0, 1)
-        index(0, [2, 1, 0, 3])
-        if vg[0]:
-            gather(0, 1, vg[0], 1.0, "V")
+        index(0, [[2], [1], [0], [3]])
         neighbours(t, 1, NCH)
-
-        def scalars(c):
-            if style[c]:
-                sg = [h for h in range(2) if h not in vg[c]]
-                neg2 = -1.0 if t == 3 else 1.0
-                seq = [(2, [0, 1], neg2), (1, sg, 1.0), (0, [0, 1], -neg2), (3, [0, 1], -1.0)]
-            elif c == NCH - 1:
-                seq = [(al, [h], 1.0) for h, als in (([1, [1, 0, 2, 3]], [0, [0, 2, 3]]) if t < 3 else ([1, [1, 3, 0, 2]], [0, [3, 0, 2]])) for al in als]
-            elif t < 3:
-                seq = [(0, [0, 1], 1.0), (1, [1], 1.0), (2, [0, 1], 1.0), (3, [0, 1], 1.0)]
-            else:
-                seq = [(3, [0, 1], 1.0), (1, [1], 1.0), (0, [0, 1], 1.0), (2, [0, 1], 1.0)]
-            for al, hs, sign in seq:
-                if hs:
-                    gather(c, al, hs, sign)
-
-        def ahead(c):
-            if c == NCH or t == 3:
-                return None
-            scalars(c)
-            if style[c]:
-                return pe_diff(c, 0, 1, 2), pe_diff(c, 1, 1, 2)
-            if c == NCH - 1:
-                return pe_diff(c, 1, 1, 0), pe_diff(c, 1, 1, 2)
-            return None
-
-        first = ahead(0)
-        todo = []
+        for c in range(1, NCH):
+            index(c, [[0, 1, 2, 3]])
         for c in range(NCH):
-            last = c == NCH - 1
-            if t == 3:
-                scalars(c)
-            carry, todo = todo, (post(t, c - 1) if c else [])
-            late = t == 0 and c == 1
-            before = [style[c - 1] if c else 0]
-
-            def nxt(n=1, force=False):
-                if late and not force:
-                    return
-                while carry:
-                    carry.pop(0)()
-                if before[0]:
-                    before[0] = 0
-                    sums(t, c - 1)
-                for _ in range(n):
-                    if todo:
-                        todo.pop(0)()
-
-            for c2 in AHEAD[c]:
-                index(c2)
-            if not last and vg[c + 1]:
-                gather(c + 1, 1, vg[c + 1], 1.0, "V")
-
-            if style[c] and t < 3:
-                b0, b1 = first
-                added(c, 0, 1, 0)
-                b2 = pe_diff(c, 0, 3, 0, flip, True)
-                b3 = pe_diff(c, 1, 3, 0, flip, True)
-                added(c, 1, 2, 3)
-                scan(c, 1, 0, b0, True)
-                scan(c, 1, 1, b1, True)
-                nxt()
-                if late:
-                    first = ahead(c + 1)
-                    op("V", cp(T.sq[:], T.sw[:].indirect(T.cand16[:])), r=["sw", "cand16"], w=["sq"])
-                    self_list()
-                    self_gather()
-                scan(c, 3, 0, b2, True)
-                nxt(2)
-                if not late:
-                    first = ahead(c + 1)
-                scan(c, 3, 1, b3, True)
-                nxt(2)
-                if late:
-                    self_gaps(t)
-            elif style[c]:
-                added(c, 0, 0, 2)
-                added(c, 1, 1, 3)
-                nxt(6)
-            elif t < 3 and last:
-                b0, b1 = first
-                b2 = narrowed(0, pe_diff(c, 1, 2, 3))
-                b3 = narrowed(1, pe_diff(c, 1, 3, 0, flip))
-                scan(c, 0, 1, b0, False)
-                scan(c, 1, 1, b1, True)
-                f0 = fused(c, 0, 0, T.fa, "fa")
-                nxt()
-                scan(c, 2, 1, b2, True)
-                nxt(2)
-                scan(c, 3, 1, b3, True)
-                b4 = narrowed(2, pe_diff(c, 0, 2, 3))
-                nxt(2)
-                b5 = pe_diff(c, 0, 3, 0, flip)
-                scan(c, 0, 0, f0, False)
-                f1 = fused(c, 0, 2, T.fb, "fb")
-                nxt()
-                code_sums(t + 1, 0, NCH - 1)
-                scan(c, 1, 0, f1, True)
-                scan(c, 2, 0, b4, True)
-                nsig[t + 1] += send_codes(t + 1, 0, NCH - 1)
-                scan(c, 3, 0, b5, True)
-            elif t < 3:
-                b0 = pe_diff(c, 1, 1, 0)
-                f0 = fused(c, 0, 0, T.fa, "fa")
-                scan(c, 0, 0, f0, False)
-                b1 = pe_diff(c, 1, 1, 2)
-                f1 = fused(c, 0, 2, T.fb, "fb")
-                nxt()
-                scan(c, 0, 1, b0, False)
-                nxt(2)
-                b2 = pe_diff(c, 0, 2, 3)
-                scan(c, 1, 1, b1, True)
-                nxt(2)
-                scan(c, 1, 0, f1, True)
-                b3 = pe_diff(c, 0, 3, 0, flip)
-                scan(c, 2, 0, b2, True)
-                nxt()
-                b4 = pe_diff(c, 1, 2, 3)
-                scan(c, 3, 0, b3, True)
-                b5 = pe_diff(c, 1, 3, 0, flip)
-                scan(c, 2, 1, b4, True)
-                scan(c, 3, 1, b5, True)
-                first = ahead(c + 1)
-            else:
-                b0 = pe_diff(c, 1, 1, 3)
-                b1 = pe_diff(c, 1, 0, 2)
-                scan(c, 1, 1, b0, True)
-                scan(c, 3, 1, b0, False)
-                nxt()
-                scan(c, 0, 1, b1, True)
-                scan(c, 2, 1, b1, False)
-                nxt(2)
-                f0 = fused(c, 0, 3, T.fa, "fa")
-                nxt(3)
-                scan(c, 1, 0, f0, True)
-                scan(c, 3, 0, f0, False)
-                b2 = pe_diff(c, 0, 0, 2)
-                scan(c, 0, 0, b2, True)
-                scan(c, 2, 0, b2, False)
-                if last:
-                    dma("Y", T.yg[:, 0:384], T.ygb[:, 0:48, :], r=["yg%d%d" % (i, k) for i in range(3) for k in range(8)])
-                    dma("Y", T.yc[:, 0:384], T.ycb[0:128:16, 0:48, :], r=["yc%d%d" % (i, k) for i in range(3) for k in range(8)])
-            if late or last or not style[c]:
-                nxt(6, True)
-        for st in post(t, NCH - 1):
-            st()
+            now[0] = c
+            sets = chunk(t, c)
+            if t == 3 and c == 3:
+                dma("Y", T.yg[:, 0:384], T.ygb[:, 0:48, :], r=["yg%d" % i for i in range(3)])
+                dma("Y", T.yc[:, 0:384], T.ycb[0:128:16, 0:48, :], r=["yc%d" % i for i in range(3)])
+            post(t, c, sets)
+            if t < 3 and c == 2:
+                places(0, 3)
+                send_codes(t + 1, 0, 3)
+        now[0] = 0
         if t < 3:
-            code_sums(t + 1, NCH - 1, NCH)
-            nsig[t + 1] += send_codes(t + 1, NCH - 1, NCH)
+            places(3, 4)
+            send_codes(t + 1, 3, 4)
             own_codes(t + 1)
-            self_list()
-            self_gather()
             self_gaps(t + 1)
-            if t == 2:
-                code_rows(3)
-                last_constants()
+        if t == 2:
+            code_rows()
+            op("V", ts(T.bn[:], T.bm[:], -4096.0, A.mult), r=["bm"], w=["bn"])
+            op("V", ts(fcol(14), fcol(0), 0.0, A.is_equal, 65536.0, A.mult), r=["cf0"], w=["cf14"])
+            op("V", ts(fcol(15), fcol(0), 1.0, A.is_equal), r=["cf0"], w=["cf15"])
+            op("V", tt(fcol(14), fcol(14), fcol(15), A.subtract), r=["cf14", "cf15"], w=["cf14"])
+            op("V", ts(T.kc[:], T.ones[:], fcol(14), A.mult), r=["ones", "cf14"], w=["kc"])
     dma("Y", T.yg[:, 384:512], T.ygb[:, 48:64, :], r=["yg3%d" % k for k in range(8)])
     dma("S", T.yc[:, 384:512], T.ycb[0:128:16, 48:64, :], r=["yc3%d" % k for k in range(8)])
+
+    seq, banks = order(prog)
+    where.update(banks)
+    for i in seq:
+        prog[i]["emit"]()
     g.wait_ge(T.sem.loc, sum(nsig))
     for e in ("sV", "sS", "sP", "sG"):
         if know["Y"].get(e, 0) < count[e]:

from concourse.bass import DstId, RemoteDMATransfer
from concourse.mybir import AluOpType, ActivationFunctionType

BF, F32, I32, U16 = "bfloat16", "float32", "int32", "uint16"
NCH = 4
BIG = 1024.0
MODE = ["PAAP", "AAAP", "AAAP", "AAAA"]
VG = [[[(1, 0), (1, 1)], [(1, 0), (1, 1)], [(1, 0), (2, 0)], [(2, 1)]],
      [[(1, 0), (0, 0), (0, 1)], [(1, 0), (2, 0)], [(2, 1), (0, 0), (0, 1)], [(1, 0)]],
      [[(0, 0), (0, 1)], [(1, 0), (3, 0), (2, 0)], [(2, 1), (0, 1)], [(1, 0)]],
      [[(1, 0), (1, 1), (0, 0)], [(1, 0), (2, 0)], [(1, 0), (2, 1)], [(1, 0), (0, 1)]]]
NAR = [[[(1, 0), (0, 0)], [], [(3, 1)], [(2, 1), (3, 1)]],
       [[(3, 1)], [(1, 0)], [(1, 1)], [(2, 1), (0, 0), (0, 1), (3, 1)]],
       [[(3, 1)], [(3, 0)], [], [(2, 1), (3, 1), (0, 1), (3, 0)]],
       [[], [], [], []]]
FIRSTH = [1, 1, 0, 0]
LASTHALF = [[3, 0], [3, 2], [3], []]
SPLIT = 1024
CYC, WAKE, EPS, GCYC, BIAS, ADDUS, DW = 1.04e-3, 0.06, 0.1, 1.6, 3.0, 2.2, 0.5
NND, NNF, NDMA = 4, 4, 12
SCRATCH = {
    "pw": ("sbuf", [128, 4096], BF), "sw": ("sbuf", [128, 4096], I32), "sq": ("sbuf", [128, 1792], F32),
    "cq": ("sbuf", [128, 1792], BF),
    "candl": ("sbuf", [128, 112], I32), "clo": ("sbuf", [128, 112], I32), "clob": ("sbuf", [128, 112], BF),
    "chib": ("sbuf", [128, 112], BF), "cand16": ("sbuf", [128, 112], U16),
    "nbi": ("sbuf", [128, 16], I32), "nbu": ("sbuf", [128, 16], U16), "geoi": ("sbuf", [128, 16], I32),
    "geof": ("sbuf", [128, 16], F32), "gm": ("sbuf", [128, 256], F32), "geor": ("sbuf", [128, 16, 4, 16], F32),
    "w0": ("sbuf", [128, 256], F32), "w1": ("sbuf", [128, 256], F32), "w2": ("sbuf", [128, 256], F32), "w3": ("sbuf", [128, 256], F32),
    "ones": ("sbuf", [128, 128], BF), "ip": ("sbuf", [128, 128], BF), "im": ("sbuf", [128, 128], BF),
    "bt": ("sbuf", [128, 128], BF), "bm": ("sbuf", [128, 128], BF), "bf32": ("sbuf", [128, 128], F32), "bn": ("sbuf", [128, 128], BF),
    "kc": ("sbuf", [128, 128], BF), "selk": ("sbuf", [128, 64, 2], BF), "csel": ("sbuf", [128, 8, 8, 8, 2], BF), "casel": ("sbuf", [128, 2, 64, 2], BF),
    "thr": ("sbuf", [128, 128], F32), "qrow": ("sbuf", [128, 128], F32), "m16": ("sbuf", [128, 16], F32),
    "rt0": ("sbuf", [128, 24], BF), "rt1": ("sbuf", [128, 24], BF), "rt2": ("sbuf", [128, 24], BF),
    "rmin": ("sbuf", [128, 512], BF), "rmax": ("sbuf", [128, 512], BF),
    "ci": ("sbuf", [128, 16], I32), "cf": ("sbuf", [128, 16], F32),
    "posc": ("sbuf", [128, 4, 8], F32), "headc": ("sbuf", [128, 4, 8], F32), "sbase": ("sbuf", [128, 4, 8], F32), "sbf": ("sbuf", [128, 4, 8], F32),
    "t1": ("sbuf", [128, 4, 8], F32), "t3": ("sbuf", [128, 4, 8], F32), "offc": ("sbuf", [128, 32], U16), "offs": ("sbuf", [128, 32], U16),
    "crow": ("sbuf", [128, 4, 128], BF), "own": ("sbuf", [128, 512], F32), "ns": ("sbuf", [128, 4, 8, 16], F32), "cr": ("sbuf", [128, 8, 16], F32),
    "nsx": ("sbuf", [128, 4, 16, 8], F32), "crx": ("sbuf", [128, 4, 16, 8], F32),
    "cn": ("sbuf", [128, 256], F32), "idx": ("sbuf", [128, 16, 4, 16], I32), "off": ("sbuf", [128, 1024], U16),
    "ygb": ("sbuf", [128, 64, 8], F32), "ycb": ("sbuf", [128, 64, 8], F32),
    "d0": ("psum", [128, 512], F32), "d1": ("psum", [128, 512], F32), "d2": ("psum", [128, 512], F32), "d3": ("psum", [128, 512], F32),
    "ca0": ("psum", [128, 2, 4, 64], F32), "ca1": ("psum", [128, 2, 4, 64], F32),
    "jb": ("psum", [128, 4, 8, 16], F32), "mb": ("psum", [128, 4, 128], F32),
}
for _c in range(NCH):
    SCRATCH["e%d" % _c] = ("sbuf", [128, 4096], BF)
    SCRATCH["sc%d" % _c] = ("sbuf", [128, 8, 512], BF)
    SCRATCH["flg%d" % _c] = ("sbuf", [128, 128], BF)
    SCRATCH["dm%d" % _c] = ("sbuf", [128, 128], BF)
    SCRATCH["n%d" % _c] = ("sbuf", [128, 512], BF)
    SCRATCH["f%d" % _c] = ("sbuf", [128, 512], BF)
SEMAPHORES = ["sV", "sS", "sP", "sG", "loc"] + ["arr%d" % i for i in range(4)] + ["dma%d" % i for i in range(NDMA)] + ["add%d" % i for i in range(8)]


def slot(t, al, b):
    s = t + 1
    if s in (2, 4):
        return 2 * al + b
    return (s * al + 4 * b) % 8


def order(prog):
    n = len(prog)
    wr, rd, users = {}, {}, {}
    succs, left = [[] for _ in range(n)], []
    for i, p in enumerate(prog):
        s = set(wr[k] for k in p["r"] + p["w"] if k in wr)
        for k in p["w"]:
            s.update(rd.get(k, ()))
        s.discard(i)
        for k in p["r"]:
            rd.setdefault(k, []).append(i)
        for k in p["w"]:
            wr[k] = i
            rd[k] = []
        left.append(len(s))
        for q in s:
            succs[q].append(i)
        for v in p["use"]:
            users[v] = users.get(v, 0) + 1
    path = [0.0] * n
    for i in range(n - 1, -1, -1):
        p = prog[i]
        path[i] = p["us"] + p["lat"] + (p["dma"] * DW + 1.8 if p["dma"] else 0.0) + max([path[q] + WAKE for q in succs[i]] or [0.0])
    rank = [path[i] - BIAS * prog[i]["c"] for i in range(n)]
    at = [0.0] * n
    ready = [i for i in range(n) if not left[i]]
    qfree, bank, engines = {}, {}, 0.0
    free = {k: 0.0 for k in range(4)}
    where, seq = {}, []
    while ready:
        cand = []
        for i in ready:
            p = prog[i]
            t = max(at[i], qfree.get(p["e"], 0.0))
            if p["alloc"] is not None:
                if not free:
                    continue
                t = max(t, min(free.values()) + WAKE)
            for b in p["x"]:
                if b in bank and bank[b][0] != p["e"]:
                    t = max(t, bank[b][1] + WAKE)
            cand.append((t, i))
        best, i = min(cand)
        e = prog[i]["e"]
        t, i = max([c for c in cand if prog[c[1]]["e"] == e and c[0] <= best + EPS], key=lambda c: (rank[c[1]], -c[1]))
        p = prog[i]
        if p["alloc"] is not None:
            k = min(free, key=lambda b: free[b])
            where[p["alloc"]] = k
            del free[k]
        qfree[e] = t + p["us"]
        if p["dma"]:
            engines = max(t + 1.2, engines) + p["dma"]
            end = engines + .6
        else:
            end = t + p["us"] + p["lat"]
        for b in p["x"]:
            bank[b] = (e, end)
        for v in p["use"]:
            users[v] -= 1
            if not users[v]:
                free[where[v]] = end
        ready.remove(i)
        seq.append(i)
        for q in succs[i]:
            left[q] -= 1
            at[q] = max(at[q], end + WAKE)
            if not left[q]:
                ready.append(q)
    assert len(seq) == n
    return seq, where


def rank_program(g, core, T, topo):
    rank = T.rank_of(core)
    if rank is None:
        return
    A = AluOpType
    COPY = ActivationFunctionType.Copy
    V, S, P = g.vector, g.scalar, g.tensor
    queue = {"V": V, "S": S, "P": P, "G": g, "Y": g.sync}

    prog = []
    now = [0]
    where = {}

    def rec(e, emit, r, w, x, us, lat=0.0, load=0.0, use=(), alloc=None):
        prog.append({"e": e, "emit": emit, "r": list(r), "w": list(w), "x": list(x), "us": us, "lat": lat, "dma": load, "use": list(use), "alloc": alloc, "c": now[0]})

    def op(e, calls, r=(), w=(), x=(), n=64, us=None, use=(), alloc=None, pre=None):
        calls = calls if isinstance(calls, list) else [calls]

        def emit():
            if pre:
                pre()
            xs = list(x) + ["d%d" % where[v] for v in list(use) + ([alloc] if alloc is not None else [])]
            need(e, deps(e, r, w, xs))
            sem = "s" + e
            for call in calls:
                call().then_inc(T.sem[sem], 1)
                count[sem] += 1
            done(e, sem, count[sem], r, w, xs)
        rec(e, emit, r, w, x, max(64, n) * CYC if us is None else us, 0.0, 0.0, use, alloc)

    def dma(e, out, in_, r=(), w=(), load=0.5):
        def emit():
            need(e, deps("dma", r, w, ()))
            sem = "dma%d" % ndma[0]
            ndma[0] += 1
            queue[e].dma_start(out, in_).then_inc(T.sem[sem], 16)
            done(e, sem, 16, r, w)
        rec(e, emit, r, w, (), .1, 0.0, load)

    nadd = [0] * 8

    def dma_add(i, out, in_, r, w):
        def emit():
            need("G", deps("dma", r, w, ()))
            nadd[i] += 16
            g.dma_start(out, in_, accum_op=A.add).then_inc(T.sem["add%d" % i], 16)
            done("G", "add%d" % i, nadd[i], r, w)
        rec("G", emit, r, w, (), 1.0, 0.0, ADDUS)

    count = {"sV": 0, "sS": 0, "sP": 0, "sG": 0}
    know = {e: {} for e in queue}
    snaps = {}
    wr, rd, bank = {}, {}, {}
    ndma = [0]

    def need(e, tokens):
        todo = {}
        for sem, val in tokens:
            if know[e].get(sem, 0) < val:
                todo[sem] = max(todo.get(sem, 0), val)
        items = sorted(todo.items(), key=lambda it: -sum(snaps[it].values()))
        for sem, val in items:
            if know[e].get(sem, 0) >= val:
                continue
            queue[e].wait_ge(T.sem[sem], val)
            for k, v in snaps[(sem, val)].items():
                know[e][k] = max(know[e].get(k, 0), v)
            know[e][sem] = max(know[e].get(sem, 0), val)

    def deps(e, r, w, x):
        own = "s" + e
        tok = [wr[k] for k in list(r) + list(w) if k in wr]
        for k in w:
            tok += [q for q in rd.get(k, ()) if q[0] != own]
        for k in x:
            tok += [q for q in bank.get(k, {}).values() if q[0] != own]
        return tok

    def done(e, sem, val, r, w, x=()):
        sn = dict(know[e])
        sn[sem] = val
        snaps[(sem, val)] = sn
        tok = (sem, val)
        for k in r:
            rd[k] = [q for q in rd.get(k, []) if q[0] != sem] + [tok]
        for k in w:
            wr[k] = tok
            rd[k] = []
        for k in x:
            bank.setdefault(k, {})[sem] = tok

    W = [T.w0, T.w1, T.w2, T.w3]
    D = [T.d0, T.d1, T.d2, T.d3]
    E = [T["e%d" % c] for c in range(NCH)]
    SC = [T["sc%d" % c] for c in range(NCH)]
    RT = [T.rt0, T.rt1, T.rt2]
    CA = [T.ca0, T.ca1]
    others = [c for c in T.cores if c != core]

    def ts(out, in0, s1, op0, s2=None, op1=None):
        if op1 is None:
            return lambda: V.tensor_scalar(out, in0, s1, None, op0)
        return lambda: V.tensor_scalar(out, in0, s1, s2, op0, op1)

    def tt(out, a, b, o):
        return lambda: V.tensor_tensor(out, a, b, o)

    def cp(out, a):
        return lambda: V.tensor_copy(out, a)

    def ms(out, v):
        return lambda: V.memset(out, v)

    def mm(out, l, rhs, st, sp):
        return lambda: P.matmul(out, l, rhs, st, sp)

    def gat(n):
        return .05 + GCYC * CYC * n

    dma("Y", T.candl[:], T.cand[:], w=["candl"])
    dma("Y", T.pw[:, 0:SPLIT], T.pe[:, 0:SPLIT], w=["pwa", "yq"], load=1.0)
    dma("S", T.geoi[:], T.geo[:], w=["geoi"])
    dma("S", T.nbi[:], T.nb[:], w=["nbi"])

    ci, cf = T.ci, T.cf

    def icol(k):
        return ci[:, k:k + 1]

    def fcol(k):
        return cf[:, k:k + 1]

    FREE = {"allow_small_or_imprecise_dtypes": True}
    op("G", lambda: g.iota(icol(0), [[0, 1]], 0, 1), w=["ci0"], us=.13)
    op("G", lambda: g.iota(T.posc[:], [[448, 4], [1, 8]], 0, 0, **FREE), w=["posc0", "posc3"], us=.2)
    op("V", ms(T.ones[:], 1.0), w=["ones"])
    op("V", ms(T.cq[:], 0.0), w=["cq"], n=896)
    op("G", lambda: g.affine_select(T.bt[:], T.ones[:], [[-16, 8], [0, 16]], A.is_ge, 0.0, 0, 1), r=["ones"], w=["bt"], us=.43)
    op("G", lambda: g.affine_select(T.bm[:], T.bt[:], [[16, 8], [0, 16]], A.is_ge, 0.0, 15, -1), r=["bt"], w=["bm"], us=.43)
    op("G", lambda: g.iota(T.qrow[:], [[0, 8], [1, 16]], 0, 0, **FREE), w=["qrow"], us=.4)
    op("G", lambda: g.affine_select(T.ip[:], T.ones[:], [[-1, 128]], A.is_equal, 0.0, 0, 1), r=["ones"], w=["ip"], us=.43)
    op("G", lambda: g.iota(T.headc[:], [[448, 4], [0, 8]], 8, 0, **FREE), w=["headc0", "headc3"], us=.2)
    op("G", lambda: g.iota(T.sbase[:], [[-7164, 4], [0, 8]], 0, 0, **FREE), w=["sbase"], us=.2)
    op("V", ts(icol(1), icol(0), 15, A.bitwise_and), r=["ci0"], w=["ci1"])
    op("V", cp(fcol(1), icol(1)), r=["ci1"], w=["cf1"])
    op("V", ts(fcol(2), fcol(1), 28.0, A.mult), r=["cf1"], w=["cf2"])
    op("V", ts(fcol(3), fcol(1), 1.5, A.is_lt), r=["cf1"], w=["cf3"])
    op("V", ts(T.posc[:], T.posc[:], fcol(2), A.add), r=["posc0", "posc3", "cf2"], w=["posc0", "posc3"])
    op("V", ts(T.clo[:], T.candl[:], 63, A.bitwise_and), r=["candl"], w=["clo"], n=112)
    op("V", tt(T.chib[:], T.candl[:], T.clo[:], A.subtract), r=["clo", "candl"], w=["chib"], n=224)
    op("V", cp(T.clob[:], T.clo[:]), r=["clo"], w=["clob"], n=112)
    dma("Y", T.cq[0:128:16, :], T.chib[:], r=["chib", "cq", "yq"], w=["cqh", "cqw"])
    dma("Y", T.cq[1:128:16, :], T.clob[:], r=["clob", "cq", "yq"], w=["cql", "cqv"])
    dma("Y", T.pw[:, SPLIT:4096], T.pe[:, SPLIT:4096], w=["pw", "cqw"], load=2.4)
    dma("Y", T.sw[:], T.se[:], w=["sw", "cqw"], load=6.5)
    op("V", ms(T.csel[:], 0.0), w=["csel"], n=512)
    op("V", ms(T.casel[:], 0.0), w=["casel"], n=128)
    op("V", ts(T.selk[:], T.bm[:], fcol(3), A.mult), r=["bm", "cf3"], w=["selk"])
    op("V", ts(T.m16[:], T.qrow[:, 0:16], fcol(1), A.is_equal), r=["qrow", "cf1"], w=["m16"])
    op("V", cp(T.geof[:], T.geoi[:]), r=["geoi"], w=["geof"])
    op("V", cp(T.bf32[:], T.bm[:]), r=["bm"], w=["bf32"], n=128)
    for u in range(8):
        op("V", cp(T.csel[:, u, :, u, :], T.selk[:, u:64:8, :]), r=["selk", "csel"], w=["cselu%d" % u])
    for b in range(2):
        op("V", cp(T.casel[:, b, :, b], T.selk[:, :, b]), r=["selk", "casel"], w=["caselb%d" % b])
    GM = ["gm%d%d" % (c, j) for c in range(NCH) for j in range(4)]
    for c in range(NCH):
        for j in range(4):
            lo = 64 * c + 16 * j
            op("V", ts(T.gm[:, lo:lo + 16], T.m16[:], T.geof[:, 4 * j + c:4 * j + c + 1], A.mult), r=["m16", "geof"], w=["gm%d%d" % (c, j)])
    op("P", mm(T.jb[:, 2:4, :, :], T.bf32[:], T.gm[:], True, True), r=["bf32"] + GM, w=["jbg"], x=["jb"], us=.8)
    for c in range(NCH):
        for al in range(4):
            o, i = T.geor[:, 4 * c + al, :, :], T.jb[:, 2 + c // 2, 4 * (c % 2):4 * (c % 2) + 4, :]
            op("S", lambda o=o, i=i: S.activation(o, i, COPY, bias=-65536.0, scale=16.0), r=["jbg"], w=["geor%d" % (4 * c + al)], x=["jb"])

    def crow_of(a, t, c0=0, c1=NCH):
        return T.crow[:, c0:c1, 16 * a:16 * a + 16] if t else T.cq[:, a:1792:28]

    def crow_keys(t, c0=0, c1=NCH):
        return ["crow%d" % c for c in range(c0, c1)] if t else ["cq", "cqh", "cql"]

    nsig = [0] * 4

    def send_codes(t, c0, c1):
        op("P", [mm(T.jb[:, 1, c0:c1, :], T.csel[:, u, :, :, :], crow_of(u, t, c0, c1), u == 0, u == 7) for u in range(8)],
           r=crow_keys(t, c0, c1) + ["cselu%d" % u for u in range(8)], w=["jbc"], x=["jb"], us=.35)
        mine = W[t][:, 64 * rank + 16 * c0:64 * rank + 16 * c1]
        key = "wown%d%d" % (t, c0)
        op("V", cp(mine, T.jb[:, 1, c0:c1, :]), r=["jbc"], w=[key], x=["jb"])

        def emit():
            need("G", deps("G", [key], [], []))
            m = topo.mask(core, others[0])
            ids = []
            for o in others:
                m &= topo.mask(core, o)
                a = topo.addr(o)
                ids.append(DstId(rid=a[0], pnc=a[1]))
            tr = RemoteDMATransfer(dst_ids=ids, dma_engine_mask=m, remote_sem=T.sem["arr%d" % t], srcs=[mine], dsts=[mine for _ in ids])
            g.remote_dma_fused([tr], local_sem=T.sem.loc)
            nsig[t] += bin(m).count("1")
        rec("G", emit, [key], ["sent%d%d" % (t, c0)], [], .6, 3.0 if t else 5.0)

    def own_codes(t):
        for al in range(4):
            calls = [mm(CA[al // 2][:, al % 2, j, :], T.casel[:, b, :, :], crow_of(slot(t, al, b), t), b == 0, b == 1) for j in range(4) for b in range(2)]
            op("P", calls, r=crow_keys(t) + ["caselb0", "caselb1"], w=["ca%d" % al] + ["pr%d" % (4 * c + al) for c in range(NCH)], x=["cab%d" % (al // 2)], us=.35)

    def self_gaps(t):
        op("V", ts(T.sbf[:], T.posc[:], 16.0, A.mult), r=["posc0", "posc3"], w=["sbf"])
        op("V", tt(T.sbf[:], T.sbf[:], T.sbase[:], A.add), r=["sbf", "sbase"], w=["sbf"])
        for c in range(NCH):
            op("V", cp(T.offs[:, c:32:4], T.sbf[:, c, :]), r=["sbf"], w=["offs%d" % c])
        op("S", lambda: S.activation(T.own[:], T.sq[:].indirect(T.offs[:]), COPY), r=["sq"] + ["offs%d" % c for c in range(NCH)], w=["own"], us=gat(512))
        for k in range(8):
            a = slot(t, k // 2, k % 2)
            b = (a + 1 + t) % 8
            if t < 3:
                op("V", tt(T.ns[:, :, k, :], T.own[:, 64 * b:64 * b + 64], T.own[:, 64 * a:64 * a + 64], A.subtract), r=["own"], w=["ns%d" % k], n=128)
            else:
                op("V", tt(T.nsx[:, 0:3, :, k], T.own[:, 64 * b:64 * b + 48], T.own[:, 64 * a:64 * a + 48], A.subtract), r=["own"], w=["nsx%d" % k], n=96)
                op("V", tt(T.ns[:, 3, k, :], T.own[:, 64 * b + 48:64 * b + 64], T.own[:, 64 * a + 48:64 * a + 64], A.subtract), r=["own"], w=["ns%d" % k])

    NS = ["ns%d" % k for k in range(8)]
    NX = ["nsx%d" % k for k in range(8)]
    MB = ["mbp%d" % c for c in range(NCH)]

    def code_rows():
        op("P", [mm(T.mb[:], T.selk[:], T.crow[:], True, True)], r=crow_keys(3) + ["selk"], w=MB, x=["mb"], us=.3)
        for a in range(8):
            op("V", cp(T.crx[:, 0:3, :, a], T.mb[:, 0:3, 16 * a:16 * a + 16]), r=MB, w=["crx%d" % a], x=["mb"])
            op("V", cp(T.cr[:, a, :], T.mb[:, 3, 16 * a:16 * a + 16]), r=MB, w=["cr%d" % a], x=["mb"])

    waited = {}

    def neighbours(t, c0, c1):
        def pre():
            if t not in waited:
                waited[t] = 1
                V.wait_ge(T.sem["arr%d" % t], 3 * nsig[t])
        op("V", cp(T.cn[:, 64 * c0:64 * c1], W[t][:].indirect(T.nbu[:, 4 * c0:4 * c1])), r=["nbu", "wown%d0" % t, "wown%d3" % t, "sent%d0" % t, "sent%d3" % t],
           w=["cn%d" % c for c in range(c0, c1)], us=gat(64 * (c1 - c0)), pre=pre)

    def index(c, groups):
        for als in groups:
            ks = [4 * c + al for al in als]
            for al in als:
                ca = CA[al // 2][:, al % 2, :, 16 * c:16 * c + 16]
                op("V", tt(ca, T.cn[:, 64 * c:64 * c + 64], ca, A.mult), r=["cn%d" % c, "ca%d" % al], w=["pr%d" % (4 * c + al)], x=["cab%d" % (al // 2)])
            for al in als:
                k = 4 * c + al
                ca = CA[al // 2][:, al % 2, :, 16 * c:16 * c + 16]
                op("V", tt(T.idx[:, k, :, :], ca, T.geor[:, k, :, :], A.add), r=["pr%d" % k, "geor%d" % k], w=["ix%d" % k], x=["cab%d" % (al // 2)])
            IX = ["ix%d" % k for k in ks]
            v = T.idx[:, ks[0]:ks[-1] + 1, :, :]
            op("V", ts(v, v, 4, A.arith_shift_right, 4095, A.bitwise_and), r=IX, w=IX, n=64 * len(ks))
            op("V", cp(T.off[:, 64 * ks[0]:64 * ks[-1] + 64], v), r=IX, w=["of%d" % k for k in ks], n=64 * len(ks))

    def gather(c, al, hs, sign=1.0, e="S"):
        k = 4 * c + al
        lo, n = 64 * k + 32 * hs[0], 32 * len(hs)
        out, src = E[c][:, 16 * lo - 4096 * c:16 * (lo + n) - 4096 * c], T.pw[:].indirect(T.off[:, lo:lo + n])
        if e == "V":
            call = cp(out, src) if sign == 1.0 else ts(out, src, sign, A.mult)
        else:
            call = lambda: S.activation(out, src, COPY, scale=sign)
        op(e, call, r=["pw", "pwa", "of%d" % k], w=["e%d%d%d" % (c, al, h) for h in hs], us=gat(16 * n))

    def added(c, i, into, what):
        p, q = 1024 * into, 1024 * what
        dma_add(2 * c + i, E[c][:, p:p + 1024], E[c][:, q:q + 1024], ["e%d%d%d" % (c, what, h) for h in range(2)], ["e%d%d%d" % (c, into, h) for h in range(2)])

    def held(c, al, h):
        return (E[c], "e%d%d%d" % (c, al, h), 0, 1024 * al + 512 * h)

    nv, nn, nf = [0], [0], [0]

    def bank_diff(terms, r):
        v = nv[0]
        nv[0] += 1

        def call(j, b, i):
            buf, col, fl, sg = terms[i]
            lo = col + 256 * j
            rhs = buf[:, lo + (1 - b if fl else b):lo + 256:2]
            o = 256 * j + 128 * b
            return lambda: P.matmul(D[where[v]][:, o:o + 128], (T.ip if sg > 0 else T.im)[:], rhs, i == 0, i == len(terms) - 1)
        calls = [call(j, b, i) for j in range(2) for b in range(2) for i in range(len(terms))]
        op("P", calls, r=list(r) + ["ip", "im"], w=["vd%d" % v], us=.085 * len(calls), alloc=v)
        return (v, "vd%d" % v, 1, 0)

    def narrowed(src):
        i = nn[0] % NND
        nn[0] += 1
        out, v = T["n%d" % i], src[0]
        op("S", lambda: S.activation(out[:], D[where[v]][:], COPY), r=[src[1]], w=["n%d" % i], use=[v], n=512)
        return (out, "n%d" % i, 2, 0)

    def fused(c, h, al, other):
        i = nf[0] % NNF
        nf[0] += 1
        out, key = T["f%d" % i], "f%d" % i
        k = 4 * c + al
        lo = 64 * k + 32 * h
        p = 1024 * other + 512 * h
        op("V", tt(out[:], T.pw[:].indirect(T.off[:, lo:lo + 32]), E[c][:, p:p + 512], A.subtract), r=["pw", "pwa", "of%d" % k, "e%d%d%d" % (c, other, h)], w=[key], us=gat(512))
        return (out, key, 0, 0)

    def scan(c, al, h, src, low):
        rp = T.rmin if low else T.rmax
        o0, o1 = (A.max, A.min) if low else (A.min, A.max)
        k = 4 * h + al
        if src[2] == 1:
            calls = [lambda: V.tensor_tensor_scan(SC[c][:, k, :], rp[:], D[where[src[0]]][:], 0.0, o0, o1)]
        elif src[2] == 2:
            calls = [lambda: V.tensor_tensor_scan(SC[c][:, k, :], rp[:], src[0][:], 0.0, o0, o1)]
        else:
            calls = [lambda j=j, b=b: V.tensor_tensor_scan(SC[c][:, k, 256 * j + 128 * b:256 * j + 128 * b + 128], rp[:, 0:128],
                                                           src[0][:, src[3] + 256 * j + b:src[3] + 256 * j + 256:2], 0.0, o0, o1) for j in range(2) for b in range(2)]
        op("V", calls, r=[src[1], "rmin" if low else "rmax"], w=["sc%d%d%d" % (c, al, h)], use=[src[0]] if src[2] == 1 else [], us=(512 if src[2] == 1 else 256) * CYC)

    def jsum(c, sets):
        calls = []
        for k0, k1, low in sets:
            for j in range(4):
                h, lo = 4 * (j // 2), 256 * (j % 2)
                calls.append(mm(T.jb[:, 0, 2 * k0:2 * k1, :], (T.ip if low else T.im)[:], SC[c][:, h + k0:h + k1, lo + 7:lo + 256:8], j == 0, j == 3))
        op("P", calls, r=["ip", "im"] + ["sc%d%d%d" % (c, al, h) for al in range(4) for h in range(2)], w=["jbs"], x=["jb"], us=.045 * len(calls))

    def chunk(t, c):
        flip = (t != 1)
        onv, nar = VG[t][c], NAR[t][c]
        vg = [h for h in range(2) if (1, h) in onv]
        a = MODE[t][c] == "A"
        first = [FIRSTH[t], 1 - FIRSTH[t]]
        halves = [[h] for h in first] if c in LASTHALF[t] else [[0, 1]]

        def gathers(al, hs, sign=1.0, skip=()):
            for e in "VS":
                h2 = [h for h in hs if ((al, h) in onv) == (e == "V") and h not in skip]
                if h2:
                    gather(c, al, h2, sign, e)

        def diff(k, h, p, q, sp, sq, fl=False):
            d = bank_diff([(E[c], 1024 * p + 512 * h, False, sp), (E[c], 1024 * q + 512 * h, fl, sq)], ["e%d%d%d" % (c, p, h), "e%d%d%d" % (c, q, h)])
            return narrowed(d) if (k, h) in nar else d

        if t < 3 and a:
            for al, sign in ((2, -1.0), (1, 1.0), (0, -1.0), (3, 1.0)):
                for hs in halves:
                    gathers(al, hs, sign)
            m12 = [diff(1, h, 1, 2, 1, 1) for h in range(2)]
            added(c, 0, 1, 0)
            m30 = [diff(3, h, 3, 0, 1, 1, flip) for h in range(2)]
            added(c, 1, 2, 3)
            for al, src, low in ((1, m12, True), (3, m30, True), (0, [held(c, 1, h) for h in range(2)], False), (2, [held(c, 2, h) for h in range(2)], False)):
                for h in range(2):
                    scan(c, al, h, src[h], low)
            return [(0, 1, False), (1, 2, True), (2, 3, False), (3, 4, True)]
        if t < 3:
            for hs in halves:
                for al in range(4):
                    gathers(al, hs, 1.0, vg if al == 1 else ())
            for h in first:
                if h in vg:
                    f = fused(c, h, 1, 0)
                    d = bank_diff([(f[0], 0, False, 1), (E[c], 512 * h, False, 1), (E[c], 2048 + 512 * h, False, -1)], [f[1], "e%d0%d" % (c, h), "e%d2%d" % (c, h)])
                    d = narrowed(d) if (1, h) in nar else d
                else:
                    f = diff(0, h, 1, 0, 1, -1)
                    d = None
                scan(c, 0, h, f, False)
                scan(c, 1, h, d or diff(1, h, 1, 2, 1, -1), True)
                scan(c, 2, h, diff(2, h, 2, 3, 1, -1), True)
                scan(c, 3, h, diff(3, h, 3, 0, 1, -1, flip), True)
            return [(0, 1, False), (1, 4, True)]
        gathers(3, [0, 1], 1.0 if vg else -1.0)
        gathers(1, [0, 1], 1.0, vg)
        if not vg:
            added(c, 1, 1, 3)
        gathers(2, [0, 1], -1.0)
        gathers(0, [0, 1])
        added(c, 0, 0, 2)
        for h in range(2):
            s = fused(c, h, 1, 3) if h in vg else (diff(1, h, 1, 3, 1, -1) if vg else held(c, 1, h))
            scan(c, 1, h, s, True)
            scan(c, 3, h, s, False)
        for h in range(2):
            scan(c, 0, h, held(c, 0, h), True)
            scan(c, 2, h, held(c, 0, h), False)
        return [(0, 2, True), (2, 4, False)]

    def outputs(c, sets):
        calls = []
        for k0, k1, low in sets:
            for k in range(2 * k0, 2 * k1):
                for j in range(4):
                    lo = 256 * (j % 2) + 128 * (k % 2)
                    calls.append(mm(T.mb[:, 0, k:128:8], (T.ip if low else T.im)[:], SC[c][:, 4 * (j // 2) + k // 2, lo + 7:lo + 128:8], j == 0, j == 3))
        op("P", calls, r=["ip", "im"] + ["sc%d%d%d" % (c, al, h) for al in range(4) for h in range(2)], w=["mbp0"], x=["mb"], us=.045 * len(calls))
        flg = T["flg%d" % c]
        op("V", tt(flg[:], T.mb[:, 0, :], T.nsx[:, c, :, :], A.is_gt), r=["mbp0"] + NX, w=["flg%d" % c], x=["mb"], n=128)
        op("P", [mm(T.mb[:, 1, :], T.kc[:], T.ones[:], True, False), mm(T.mb[:, 1, :], T.bn[:], flg[:], False, True)],
           r=["flg%d" % c, "bn", "kc", "ones"], w=["mbp1"], x=["mb"], us=.15)
        op("V", tt(T.ygb[:, 16 * c:16 * c + 16, :], T.mb[:, 0, :], T.nsx[:, c, :, :], A.subtract), r=["mbp0"] + NX, w=["yg%d" % c], x=["mb"], n=128)
        op("V", tt(T.ycb[:, 16 * c:16 * c + 16, :], T.mb[:, 1, :], T.crx[:, c, :, :], A.min), r=["mbp1"] + ["crx%d" % k for k in range(8)], w=["yc%d" % c], x=["mb"], n=128)

    def post(t, c, sets):
        if t == 3 and c < 3:
            outputs(c, sets)
            return
        jsum(c, sets)
        flg, dm = T["flg%d" % c], T["dm%d" % c]
        op("V", tt(flg[:], T.jb[:, 0, :, :], T.ns[:, c, :, :], A.is_gt), r=["jbs"] + NS, w=["flg%d" % c], x=["jb"], n=128)
        if t == 3:
            for k in range(8):
                op("V", tt(T.ygb[:, 16 * c:16 * c + 16, k], T.jb[:, 0, k, :], T.ns[:, c, k, :], A.subtract), r=["jbs"] + NS, w=["yg%d%d" % (c, k)], x=["jb"])
            op("P", [mm(T.mb[:, 0, :], T.kc[:], T.ones[:], True, False), mm(T.mb[:, 0, :], T.bn[:], flg[:], False, True)],
               r=["flg%d" % c, "bn", "kc", "ones"], w=["mbp0"], x=["mb"], us=.15)
            for k in range(8):
                op("V", tt(T.ycb[:, 16 * c:16 * c + 16, k], T.mb[:, 0, 16 * k:16 * k + 16], T.cr[:, k, :], A.min), r=["mbp0", "cr%d" % k], w=["yc%d%d" % (c, k)], x=["mb"])
            return
        op("P", mm(T.jb[:, 2, :, :], flg[:], T.bm[:], True, True), r=["flg%d" % c, "bm"], w=["jbg"], x=["jb"], us=.08)
        op("V", tt(dm[:], T.jb[:, 2, :, :], T.thr[:], A.is_ge), r=["jbg", "thr"], w=["dm%d" % c], x=["jb"], n=128)
        op("P", mm(T.mb[:, c, 0:24], dm[:], RT[t][:], True, True), r=["dm%d" % c, "rt%d" % t], w=["mbp%d" % c], x=["mb"], us=.06)

    def places(c0, c1):
        p, h, k = T.posc[:, c0:c1, :], T.headc[:, c0:c1, :], c0
        P3 = MB[c0:c1]
        op("V", tt(T.t1[:, c0:c1, :], T.mb[:, c0:c1, 0:8], p, A.add), r=P3 + ["posc%d" % k], w=["t1%d" % k], x=["mb"])
        op("V", tt(T.t3[:, c0:c1, :], T.mb[:, c0:c1, 8:16], h, A.add), r=P3 + ["headc%d" % k], w=["t3%d" % k], x=["mb"])
        op("V", tt(p, T.t1[:, c0:c1, :], T.t3[:, c0:c1, :], A.min), r=["t1%d" % k, "t3%d" % k], w=["posc%d" % k])
        op("V", cp(T.offc[:, 8 * c0:8 * c1], p), r=["posc%d" % k], w=["offc%d" % k])
        for c in range(c0, c1):
            op("V", cp(T.crow[:, c, :], T.cq[:].indirect(T.offc[:, 8 * c:8 * c + 8])), r=["cq", "cqh", "cql", "offc%d" % k], w=["crow%d" % c], us=gat(128))
        op("V", tt(h, T.mb[:, c0:c1, 16:24], h, A.add), r=P3 + ["headc%d" % k], w=["headc%d" % k], x=["mb"])

    send_codes(0, 0, NCH)
    own_codes(0)

    for j in range(4):
        op("V", cp(T.nbu[:, j:16:4], T.nbi[:, 4 * j:4 * j + 4]), r=["nbi"], w=["nbu"])
    op("V", ts(icol(3), icol(0), 5, A.arith_shift_right), r=["ci0"], w=["ci3"])
    op("V", ts(icol(4), icol(0), 4, A.arith_shift_right, 1, A.bitwise_and), r=["ci0"], w=["ci4"])
    op("V", ts(icol(5), icol(1), 3, A.bitwise_and), r=["ci1"], w=["ci5"])
    op("V", ts(icol(6), icol(1), 2, A.arith_shift_right), r=["ci1"], w=["ci6"])
    op("V", cp(fcol(0), icol(0)), r=["ci0"], w=["cf0"])
    for k in (3, 4, 5, 6):
        op("V", cp(fcol(k + 2), icol(k)), r=["ci%d" % k], w=["cf%d" % (k + 2)])
    op("V", ms(T.rmin[:], -BIG), w=["rmin"], n=256)
    op("V", ms(T.rmax[:], BIG), w=["rmax"], n=256)
    op("V", ts(T.im[:], T.ip[:], -1.0, A.mult), r=["ip"], w=["im"])
    op("V", ts(fcol(9), fcol(6), 4.0, A.mult), r=["cf6"], w=["cf9"])
    op("V", ts(fcol(11), fcol(5), 2.0, A.mult), r=["cf5"], w=["cf11"])
    op("V", ts(fcol(12), fcol(5), 3.0, A.mult), r=["cf5"], w=["cf12"])
    op("V", ms(T.rmin[:, 0:512:8], BIG), w=["rmin"])
    op("V", ms(T.rmax[:, 0:512:8], -BIG), w=["rmax"])
    op("V", ts(T.headc[:], T.headc[:], fcol(2), A.add), r=["headc0", "headc3", "cf2"], w=["headc0", "headc3"])
    op("V", tt(fcol(10), fcol(9), fcol(5), A.add), r=["cf9", "cf5"], w=["cf10"])
    op("V", tt(fcol(11), fcol(11), fcol(6), A.add), r=["cf11", "cf6"], w=["cf11"])
    op("V", tt(icol(7), fcol(12), fcol(9), A.add), r=["cf12", "cf9"], w=["ci7"])
    op("V", ts(icol(8), icol(7), 7, A.bitwise_and), r=["ci7"], w=["ci8"])
    op("V", cp(fcol(12), icol(8)), r=["ci8"], w=["cf12"])
    for t in range(3):
        a = fcol(10 + t)
        k = "cf%d" % (10 + t)
        op("V", ts(RT[t][:, 0:8], T.qrow[:, 0:8], a, A.is_equal, 4096.0, A.mult), r=["qrow", k], w=["rta%d" % t])
        op("V", ts(RT[t][:, 8:16], T.qrow[:, 0:8], a, A.is_gt), r=["qrow", k], w=["rtb%d" % t])
        op("V", ms(RT[t][:, 16:24], 1.0), r=["rta%d" % t, "rtb%d" % t], w=["rt%d" % t])
    op("V", ts(T.thr[:], T.qrow[:], fcol(1), A.not_equal, 1000.0, A.mult), r=["qrow", "cf1"], w=["thr"], n=128)
    op("V", ts(fcol(13), fcol(7), 448.0, A.mult), r=["cf7"], w=["cf13"])
    op("V", ts(fcol(14), fcol(1), -448.0, A.mult), r=["cf1"], w=["cf14"])
    op("V", ts(T.thr[:], T.thr[:], 15.5, A.max), r=["thr"], w=["thr"], n=128)
    op("V", tt(fcol(13), fcol(13), fcol(8), A.add), r=["cf13", "cf8"], w=["cf13"])
    op("V", cp(T.cand16[:], T.candl[:]), r=["candl"], w=["cand16"], n=112)
    op("V", tt(fcol(13), fcol(13), fcol(14), A.add), r=["cf13", "cf14"], w=["cf13"])
    op("V", ts(T.sbase[:], T.sbase[:], fcol(13), A.add), r=["sbase", "cf13"], w=["sbase"])
    op("V", cp(T.sq[:], T.sw[:].indirect(T.cand16[:])), r=["sw", "cand16"], w=["sq"], us=gat(1792))
    self_gaps(0)

    for t in range(4):
        neighbours(t, 0, 1)
        index(0, [[2], [1], [0], [3]])
        neighbours(t, 1, NCH)
        for c in range(1, NCH):
            index(c, [[0, 1, 2, 3]])
        for c in range(NCH):
            now[0] = c
            sets = chunk(t, c)
            if t == 3 and c == 3:
                dma("Y", T.yg[:, 0:384], T.ygb[:, 0:48, :], r=["yg%d" % i for i in range(3)])
                dma("Y", T.yc[:, 0:384], T.ycb[0:128:16, 0:48, :], r=["yc%d" % i for i in range(3)])
            post(t, c, sets)
            if t < 3 and c == 2:
                places(0, 3)
                send_codes(t + 1, 0, 3)
        now[0] = 0
        if t < 3:
            places(3, 4)
            send_codes(t + 1, 3, 4)
            own_codes(t + 1)
            self_gaps(t + 1)
        if t == 2:
            code_rows()
            op("V", ts(T.bn[:], T.bm[:], -4096.0, A.mult), r=["bm"], w=["bn"])
            op("V", ts(fcol(14), fcol(0), 0.0, A.is_equal, 65536.0, A.mult), r=["cf0"], w=["cf14"])
            op("V", ts(fcol(15), fcol(0), 1.0, A.is_equal), r=["cf0"], w=["cf15"])
            op("V", tt(fcol(14), fcol(14), fcol(15), A.subtract), r=["cf14", "cf15"], w=["cf14"])
            op("V", ts(T.kc[:], T.ones[:], fcol(14), A.mult), r=["ones", "cf14"], w=["kc"])
    dma("Y", T.yg[:, 384:512], T.ygb[:, 48:64, :], r=["yg3%d" % k for k in range(8)])
    dma("S", T.yc[:, 384:512], T.ycb[0:128:16, 48:64, :], r=["yc3%d" % k for k in range(8)])

    seq, banks = order(prog)
    where.update(banks)
    for i in seq:
        prog[i]["emit"]()
    g.wait_ge(T.sem.loc, sum(nsig))
    for e in ("sV", "sS", "sP", "sG"):
        if know["Y"].get(e, 0) < count[e]:
            g.sync.wait_ge(T.sem[e], count[e])
    for i in range(ndma[0]):
        g.sync.wait_ge(T.sem["dma%d" % i], 16)
